import numpy as np
import ml_dtypes


def mxq(x, axis, fmt="e4m3"):
    dtype, down = {"e4m3": (ml_dtypes.float8_e4m3fn, 7), "e5m2": (ml_dtypes.float8_e5m2, 14)}[fmt]
    v = np.moveaxis(np.asarray(x, np.float32).astype(ml_dtypes.bfloat16).astype(np.float64), axis, -1)
    blocks = v.reshape(v.shape[:-1] + (-1, 32))
    amax = np.abs(blocks).max(-1, keepdims=True)
    byte = np.maximum(np.where(amax > 0, np.frexp(amax)[1] - 1 + 127, 0) - down, 1)
    scale = np.exp2(byte - 127.0)
    codes = (blocks / scale).astype(np.float32).astype(dtype).astype(np.float64)
    return np.moveaxis((codes * scale).reshape(v.shape), -1, axis)


WIDE = False


def mx_kscale(k):
    if not WIDE:
        return np.ones(k)
    levels = np.array([10, -10, 5, -5, 0])
    if k % 512:
        return np.exp2(np.random.permutation(np.resize(levels, k // 32))).repeat(32)
    a = np.empty((k // 512, 16))
    for p in range(k // 512):
        a[p, :8] = np.random.permutation(np.resize(levels, 8))
        for g in range(8):
            far = levels[np.abs(levels - a[p, g]) >= 10]
            a[p, g + 8] = far[np.random.randint(len(far))]
    return np.exp2(a.ravel()).repeat(32)


def f64(x):
    return np.asarray(x).astype(np.float64)


def striped(idx):
    return np.tile(idx.reshape(-1, 16).T, (8, 1)).astype(np.uint16)


def unstriped(offs):
    return offs[:16].T.reshape(-1).astype(np.int64)


def pack_weight(w):
    k, n = w.shape
    w = f64(np.asarray(w, np.float32).astype(ml_dtypes.bfloat16)).reshape(k // 32, 32, n)
    amax = np.abs(w).max(1)
    byte = np.clip(np.where(amax > 0, np.frexp(amax)[1] - 1 + 127 - 7, 1), 1, 254)
    scaled = (w * np.exp2(127.0 - byte)[:, None, :]).reshape(k, n).astype(np.float32)
    words = np.ascontiguousarray(scaled.reshape(k // 512, 128, 4, n).transpose(0, 1, 3, 2)).astype(ml_dtypes.float8_e4m3fn).view(np.uint8)
    return words, np.ascontiguousarray(byte.astype(np.uint8).reshape(k // 512, 16, n))


def unpack_weight(words, scales):
    g, p, n, _ = words.shape
    vals = np.ascontiguousarray(words).view(ml_dtypes.float8_e4m3fn).astype(np.float64) * np.repeat(np.exp2(scales.astype(np.float64) - 127.0), 8, axis=1)[..., None]
    return vals.transpose(0, 1, 3, 2).reshape(g * 512, n)


def gelu(v):
    return 0.5 * v * (1.0 + np.tanh(np.sqrt(2.0 / np.pi) * (v + 0.044715 * v**3)))


K, T, S, H, N = 512, 4096, 1024, 512, 256


def setup_inputs():
    n = np.random.standard_normal
    s = mx_kscale(K)[:, None]
    u = mx_kscale(H)
    packed_xT = pack_weight(n((K, T)) * s)
    return {
        "x_words": packed_xT[0],
        "x_scales": packed_xT[1],
        "w1": (n((K, N)) / np.sqrt(2 * K) / s).astype(np.float32),
        "w2": (n((K, H)) / np.sqrt(K) / s * u).astype(np.float32),
        "w3": (n((H, N)) / np.sqrt(2 * H) / u[:, None]).astype(np.float32),
        "offs": striped(np.random.permutation(T)[:S]),
    }


def reference(x_words, x_scales, w1, w2, w3, offs):
    xq = unpack_weight(x_words, x_scales)[:, unstriped(offs)]
    h = gelu(mxq(f64(w2), 0, "e4m3").T @ xq)
    return mxq(f64(w1), 0, "e4m3").T @ xq + mxq(f64(w3), 0, "e4m3").T @ mxq(h, 0, "e4m3")

@@ -1,0 +1,189 @@
+from contextlib import ExitStack
+
+import concourse.mybir as mybir
+
+K, T, S, H, N = 512, 4096, 1024, 512, 256
+FLOPS = 2 * S * (K * H + K * N + H * N)
+
+F32 = mybir.dt.float32
+BF16 = mybir.dt.bfloat16
+I32 = mybir.dt.int32
+U32 = mybir.dt.uint32
+U16 = mybir.dt.uint16
+U8 = mybir.dt.uint8
+FP8X4 = mybir.dt.float8_e4m3fn_x4
+GELU = mybir.ActivationFunctionType.Gelu_apprx_tanh
+
+P = 128
+PACK = 4
+HALF = S // 2
+UNIT = 128
+CHUNKS = (256, 256, 256, 128, 128)
+SCALAR_SHARE = (32, 22)
+FIRST = 896
+
+
+def tile_picked_lora_gelu_p_kernel(tc, x_words, x_scales, w1, w2, w3, offs, out):
+    nc = tc.nc
+    with ExitStack() as ctx:
+        keep = ctx.enter_context(tc.tile_pool(name="keep", bufs=1))
+        reuse = ctx.enter_context(tc.tile_pool(name="reuse", bufs=1))
+        psum = ctx.enter_context(tc.psum_pool(name="psum", bufs=1))
+
+        offsets = keep.tile([P, S // 16], U16, name="offsets")
+        nc.sync.dma_start(offsets[:], offs)
+
+        scale_table = reuse.tile([P, T], U8, name="scale_table", offset=5120, align_bytes=64)
+        nc.gpsimd.memset(scale_table[:, 0 : T // 2].bitcast(I32), 0)
+        nc.vector.memset(scale_table[:, T // 2 : T].bitcast(I32), 0)
+        word_table = keep.tile([P, T], I32, name="word_table", align_bytes=64)
+        words = x_words[0].rearrange("p n t -> p (n t)").bitcast(I32)
+        nc.sync.dma_start(word_table[:, 0:FIRST], words[:, 0:FIRST])
+        nc.sync.dma_start(scale_table[0:P:8, :].bitcast(I32), x_scales[0].bitcast(I32))
+        nc.sync.dma_start(word_table[:, FIRST:T], words[:, FIRST:T])
+
+        warm = keep.tile([P, 2], F32, name="warm")
+        nc.vector.memset(warm[:, 0:1], 0.0)
+        nc.scalar.activation(warm[:, 1:2], warm[:, 0:1], GELU)
+
+        w2_rows = w2.rearrange("(p j) c -> p j c", j=PACK)
+        w2_raw = []
+        for half in range(2):
+            raw = keep.tile([P, PACK, H // 2], F32, name=f"w2_raw{half}")
+            nc.sync.dma_start(raw[:], w2_rows[:, :, half * (H // 2) : (half + 1) * (H // 2)])
+            w2_raw.append(raw)
+
+        x_scale = keep.tile([P, S], U8, name="x_scale", align_bytes=64)
+        nc.vector.memset(x_scale[:].bitcast(I32), 0)
+        spread = keep.tile([P, S], U8, name="spread", align_bytes=64)
+        nc.vector.tensor_copy(spread[:], scale_table[:].indirect(offsets[:]))
+        for r in range(4):
+            nc.sync.dma_start(x_scale[r:P:32, :].bitcast(I32), spread[8 * r : P : 32, :].bitcast(I32))
+        w3_rows = w3.rearrange("(p j) c -> p j c", j=PACK)
+        w3_raw = []
+        for r in range(2):
+            raw = reuse.tile([P, PACK, P], F32, name=f"w3_raw{r}", offset=4096 + 2048 * r, align_bytes=64)
+            nc.sync.dma_start(raw[:], w3_rows[:, :, r * P : (r + 1) * P])
+            w3_raw.append(raw)
+        w1_raw = reuse.tile([P, PACK * N], F32, name="w1_raw", offset=8192, align_bytes=64)
+        nc.sync.dma_start(w1_raw[:], w1.rearrange("(p j) c -> p (j c)", j=PACK))
+        x_code = []
+
+        def gather_words(half, tag):
+            picked = keep.tile([P, HALF], U32, name=f"x_code{half}", tag=tag, align_bytes=64)
+            cols = offsets[:, half * (HALF // 16) : (half + 1) * (HALF // 16)]
+            nc.vector.tensor_copy(picked[:], word_table[:].bitcast(U32).indirect(cols))
+            x_code.append(picked)
+
+        gather_words(0, "first_words")
+
+        def tokens(start, width):
+            half, at = divmod(start, HALF)
+            return x_code[half][:, at : at + width].bitcast(FP8X4), x_scale[:, start : start + width]
+
+        M2 = P // 2
+        w2_code = [keep.tile([P, P], U32, name=f"w2_code{t}", align_bytes=64) for t in range(PACK)]
+        w2_scale = [keep.tile([P, P], U8, name=f"w2_scale{t}", align_bytes=64) for t in range(PACK)]
+        for half in range(2):
+            w2_bf = keep.tile([P, PACK * M2 * PACK], BF16, name=f"w2_bf{half}", tag=f"w2_bf{half}", align_bytes=64)
+            dealt = w2_bf[:].rearrange("p (t m j) -> p m t j", t=PACK, j=PACK)
+            src = w2_raw[half][:].rearrange("p j (m t) -> p m t j", t=PACK)
+            cut = SCALAR_SHARE[half]
+            nc.scalar.copy(dealt[:, 0:cut], src[:, 0:cut])
+            nc.vector.tensor_copy(dealt[:, cut:M2], src[:, cut:M2])
+            cols = slice(half * M2, (half + 1) * M2)
+            for t in range(PACK):
+                nc.vector.quantize_mx(
+                    w2_code[t][:, cols].bitcast(FP8X4), w2_scale[t][:, cols],
+                    w2_bf[:, t * M2 * PACK : (t + 1) * M2 * PACK],
+                )
+        gather_words(1, "w2_bf1")
+
+        w3_bf = keep.tile([P, N * PACK], BF16, name="w3_bf", align_bytes=64)
+        for r in range(2):
+            nc.scalar.copy(
+                w3_bf[:, r * P * PACK : (r + 1) * P * PACK].rearrange("p (c i j) -> p c j i", i=4, j=PACK),
+                w3_raw[r][:].rearrange("p j (c i) -> p c j i", i=4),
+            )
+        w1_bf = keep.tile([P, N * PACK], BF16, name="w1_bf", align_bytes=64)
+        nc.vector.tensor_copy(
+            w1_bf[:].rearrange("p (c i j) -> p c j i", i=4, j=PACK),
+            w1_raw[:].rearrange("p (j c i) -> p c j i", j=PACK, i=4),
+        )
+        w3_code = reuse.tile([P, N], U32, name="w3_code", offset=8192 + 2048, align_bytes=64)
+        w3_scale = keep.tile([P, N], U8, name="w3_scale", align_bytes=64)
+        nc.vector.quantize_mx(w3_code[:].bitcast(FP8X4), w3_scale[:], w3_bf[:])
+        w1_code = keep.tile([P, N], U32, name="w1_code", align_bytes=64)
+        w1_scale = keep.tile([P, N], U8, name="w1_scale", align_bytes=64)
+        nc.vector.quantize_mx(w1_code[:].bitcast(FP8X4), w1_scale[:], w1_bf[:])
+
+        out_rows = out.rearrange("(r p) n -> p r n", p=P)
+        starts = [sum(CHUNKS[:c]) for c in range(len(CHUNKS))]
+        last = len(CHUNKS) - 1
+
+        h_all = reuse.tile([P, S * PACK], BF16, name="h_all", offset=0, align_bytes=64)
+
+        def hidden(c):
+            width = CHUNKS[c]
+            h_bf = h_all[:, starts[c] * PACK : (starts[c] + width) * PACK]
+            for u in range(width // UNIT):
+                start = starts[c] + u * UNIT
+                bank = psum.tile([P, PACK, UNIT], F32, name="h_bank", tag=f"bank{start // UNIT}")
+                code, scale = tokens(start, UNIT)
+                for t in range(PACK):
+                    nc.tensor.matmul_mx(
+                        bank[:, t, :], lhsT=w2_code[t][:].bitcast(FP8X4), lhsT_scale=w2_scale[t][:],
+                        rhs=code, rhs_scale=scale, start=True, stop=True,
+                    )
+                nc.scalar.activation(
+                    h_bf[:, u * UNIT * PACK : (u + 1) * UNIT * PACK].rearrange("p (n t) -> p n t", t=PACK),
+                    bank[:].rearrange("p t n -> p n t"),
+                    GELU,
+                )
+            return h_bf
+
+        def output(c, h_code, h_scale):
+            width = CHUNKS[c]
+            code, scale = tokens(starts[c], width)
+            accs = [psum.tile([P, width], F32, name=f"acc{r}", tag=f"bank{2 * (c % 3) + r}") for r in range(2)]
+            rows = [slice(r * P, (r + 1) * P) for r in range(2)]
+            for r in range(2):
+                nc.tensor.matmul_mx(
+                    accs[r][:], lhsT=w1_code[:, rows[r]].bitcast(FP8X4), lhsT_scale=w1_scale[:, rows[r]],
+                    rhs=code, rhs_scale=scale, start=True, stop=False,
+                )
+            for r in range(2):
+                nc.tensor.matmul_mx(
+                    accs[r][:], lhsT=w3_code[:, rows[r]].bitcast(FP8X4), lhsT_scale=w3_scale[:, rows[r]],
+                    rhs=h_code.bitcast(FP8X4), rhs_scale=h_scale, start=False, stop=True,
+                )
+            result = keep.tile([P, 2, width], F32, name=f"result{c}")
+            for r in range(2):
+                if c == 2 or (c == last and r == 1):
+                    nc.scalar.copy(result[:, r, :], accs[r][:])
+                else:
+                    nc.vector.tensor_copy(result[:, r, :], accs[r][:])
+            nc.sync.dma_start(out_rows[:, :, starts[c] : starts[c] + width], result[:])
+
+        made = [hidden(c) for c in range(len(CHUNKS))]
+
+        def quantize(c, code, scale):
+            nc.vector.quantize_mx(code.bitcast(FP8X4), scale, made[c])
+            return code, scale
+
+        early = reuse.tile([P, HALF], U32, name="h_early", offset=8192, align_bytes=64)
+        late = keep.tile([P, HALF], U32, name="h_late", align_bytes=64)
+        s0 = keep.tile([P, 256], U8, name="s0", tag="even", align_bytes=64)
+        s1 = keep.tile([P, 256], U8, name="s1", tag="odd", align_bytes=64)
+        q0 = quantize(0, early[:, 0:256], s0[:])
+        q1 = quantize(1, early[:, 256:512], s1[:])
+        output(0, *q0)
+        s2 = keep.tile([P, 256], U8, name="s2", tag="even", align_bytes=64)
+        q2 = quantize(2, late[:, 0:256], s2[:])
+        output(1, *q1)
+        s3 = keep.tile([P, 256], U8, name="s3", tag="odd", align_bytes=64)
+        q3 = quantize(3, late[:, 256:384], s3[:, 0:128])
+        q4 = quantize(4, late[:, 384:512], s3[:, 128:256])
+        output(2, *q2)
+        output(3, *q3)
+        output(4, *q4)

@@ -19,7 +19,7 @@ PACK = 4
 HALF = S // 2
 UNIT = 128
 CHUNKS = (256, 256, 256, 128, 128)
-SCALAR_SHARE = (32, 22)
+SCALAR_SHARE = 16
 FIRST = 896
 
 
@@ -27,13 +27,12 @@ def tile_picked_lora_gelu_p_kernel(tc, x_words, x_scales, w1, w2, w3, offs, out)
     nc = tc.nc
     with ExitStack() as ctx:
         keep = ctx.enter_context(tc.tile_pool(name="keep", bufs=1))
-        reuse = ctx.enter_context(tc.tile_pool(name="reuse", bufs=1))
         psum = ctx.enter_context(tc.psum_pool(name="psum", bufs=1))
 
         offsets = keep.tile([P, S // 16], U16, name="offsets")
         nc.sync.dma_start(offsets[:], offs)
 
-        scale_table = reuse.tile([P, T], U8, name="scale_table", offset=5120, align_bytes=64)
+        scale_table = keep.tile([P, T], U8, name="scale_table", align_bytes=64)
         nc.gpsimd.memset(scale_table[:, 0 : T // 2].bitcast(I32), 0)
         nc.vector.memset(scale_table[:, T // 2 : T].bitcast(I32), 0)
         word_table = keep.tile([P, T], I32, name="word_table", align_bytes=64)
@@ -52,21 +51,17 @@ def tile_picked_lora_gelu_p_kernel(tc, x_words, x_scales, w1, w2, w3, offs, out)
             raw = keep.tile([P, PACK, H // 2], F32, name=f"w2_raw{half}")
             nc.sync.dma_start(raw[:], w2_rows[:, :, half * (H // 2) : (half + 1) * (H // 2)])
             w2_raw.append(raw)
+        w3_raw = keep.tile([P, PACK * N], F32, name="w3_raw")
+        nc.sync.dma_start(w3_raw[:], w3.rearrange("(p j) c -> p (j c)", j=PACK))
+        w1_raw = keep.tile([P, PACK * N], F32, name="w1_raw", tag="w1_raw", align_bytes=64)
+        nc.sync.dma_start(w1_raw[:], w1.rearrange("(p j) c -> p (j c)", j=PACK))
 
         x_scale = keep.tile([P, S], U8, name="x_scale", align_bytes=64)
         nc.vector.memset(x_scale[:].bitcast(I32), 0)
         spread = keep.tile([P, S], U8, name="spread", align_bytes=64)
         nc.vector.tensor_copy(spread[:], scale_table[:].indirect(offsets[:]))
         for r in range(4):
-            nc.sync.dma_start(x_scale[r:P:32, :].bitcast(I32), spread[8 * r : P : 32, :].bitcast(I32))
-        w3_rows = w3.rearrange("(p j) c -> p j c", j=PACK)
-        w3_raw = []
-        for r in range(2):
-            raw = reuse.tile([P, PACK, P], F32, name=f"w3_raw{r}", offset=4096 + 2048 * r, align_bytes=64)
-            nc.sync.dma_start(raw[:], w3_rows[:, :, r * P : (r + 1) * P])
-            w3_raw.append(raw)
-        w1_raw = reuse.tile([P, PACK * N], F32, name="w1_raw", offset=8192, align_bytes=64)
-        nc.sync.dma_start(w1_raw[:], w1.rearrange("(p j) c -> p (j c)", j=PACK))
+            nc.scalar.dma_start(x_scale[r:P:32, :].bitcast(I32), spread[8 * r : P : 32, :].bitcast(I32))
         x_code = []
 
         def gather_words(half, tag):
@@ -76,52 +71,52 @@ def tile_picked_lora_gelu_p_kernel(tc, x_words, x_scales, w1, w2, w3, offs, out)
             x_code.append(picked)
 
         gather_words(0, "first_words")
+        idle_bank = psum.tile([P, HALF], F32, name="idle_bank", tag="bank7")
+        for rep in range(4):
+            nc.tensor.matmul_mx(
+                idle_bank[:], lhsT=x_code[0][:, 0:P].bitcast(FP8X4), lhsT_scale=spread[:, 0:P],
+                rhs=x_code[0][:].bitcast(FP8X4), rhs_scale=spread[:, 0:HALF], start=True, stop=True,
+            )
+        gather_words(1, "second_words")
 
         def tokens(start, width):
             half, at = divmod(start, HALF)
             return x_code[half][:, at : at + width].bitcast(FP8X4), x_scale[:, start : start + width]
 
         M2 = P // 2
-        w2_code = [keep.tile([P, P], U32, name=f"w2_code{t}", align_bytes=64) for t in range(PACK)]
-        w2_scale = [keep.tile([P, P], U8, name=f"w2_scale{t}", align_bytes=64) for t in range(PACK)]
-        for half in range(2):
-            w2_bf = keep.tile([P, PACK * M2 * PACK], BF16, name=f"w2_bf{half}", tag=f"w2_bf{half}", align_bytes=64)
-            dealt = w2_bf[:].rearrange("p (t m j) -> p m t j", t=PACK, j=PACK)
-            src = w2_raw[half][:].rearrange("p j (m t) -> p m t j", t=PACK)
-            cut = SCALAR_SHARE[half]
-            nc.scalar.copy(dealt[:, 0:cut], src[:, 0:cut])
-            nc.vector.tensor_copy(dealt[:, cut:M2], src[:, cut:M2])
-            cols = slice(half * M2, (half + 1) * M2)
-            for t in range(PACK):
-                nc.vector.quantize_mx(
-                    w2_code[t][:, cols].bitcast(FP8X4), w2_scale[t][:, cols],
-                    w2_bf[:, t * M2 * PACK : (t + 1) * M2 * PACK],
-                )
-        gather_words(1, "w2_bf1")
+        w2_bf = keep.tile([P, PACK * P * PACK], BF16, name="w2_bf", align_bytes=64)
+        dealt = w2_bf[:].rearrange("p (t m j) -> p m t j", t=PACK, j=PACK)
+        src = [raw[:].rearrange("p j (m t) -> p m t j", t=PACK) for raw in w2_raw]
+        nc.scalar.copy(dealt[:, 0:M2], src[0])
+        nc.vector.tensor_copy(dealt[:, M2 : P - SCALAR_SHARE], src[1][:, 0 : M2 - SCALAR_SHARE])
+        nc.scalar.copy(dealt[:, P - SCALAR_SHARE : P], src[1][:, M2 - SCALAR_SHARE : M2])
+        w2_code, w2_scale = [], []
+        for t in range(PACK):
+            code = keep.tile([P, P], U32, name=f"w2_code{t}", align_bytes=64)
+            scale = keep.tile([P, P], U8, name=f"w2_scale{t}", align_bytes=64)
+            nc.vector.quantize_mx(code[:].bitcast(FP8X4), scale[:], w2_bf[:, t * P * PACK : (t + 1) * P * PACK])
+            w2_code.append(code)
+            w2_scale.append(scale)
 
-        w3_bf = keep.tile([P, N * PACK], BF16, name="w3_bf", align_bytes=64)
-        for r in range(2):
-            nc.scalar.copy(
-                w3_bf[:, r * P * PACK : (r + 1) * P * PACK].rearrange("p (c i j) -> p c j i", i=4, j=PACK),
-                w3_raw[r][:].rearrange("p j (c i) -> p c j i", i=4),
+        def quantize_weight(raw, name):
+            grouped = keep.tile([P, N * PACK], BF16, name=f"{name}_bf", align_bytes=64)
+            nc.vector.tensor_copy(
+                grouped[:].rearrange("p (c i j) -> p c j i", i=4, j=PACK),
+                raw[:].rearrange("p (j c i) -> p c j i", j=PACK, i=4),
             )
-        w1_bf = keep.tile([P, N * PACK], BF16, name="w1_bf", align_bytes=64)
-        nc.vector.tensor_copy(
-            w1_bf[:].rearrange("p (c i j) -> p c j i", i=4, j=PACK),
-            w1_raw[:].rearrange("p (j c i) -> p c j i", j=PACK, i=4),
-        )
-        w3_code = reuse.tile([P, N], U32, name="w3_code", offset=8192 + 2048, align_bytes=64)
-        w3_scale = keep.tile([P, N], U8, name="w3_scale", align_bytes=64)
-        nc.vector.quantize_mx(w3_code[:].bitcast(FP8X4), w3_scale[:], w3_bf[:])
-        w1_code = keep.tile([P, N], U32, name="w1_code", align_bytes=64)
-        w1_scale = keep.tile([P, N], U8, name="w1_scale", align_bytes=64)
-        nc.vector.quantize_mx(w1_code[:].bitcast(FP8X4), w1_scale[:], w1_bf[:])
+            code = keep.tile([P, N], U32, name=f"{name}_code", align_bytes=64)
+            scale = keep.tile([P, N], U8, name=f"{name}_scale", align_bytes=64)
+            nc.vector.quantize_mx(code[:].bitcast(FP8X4), scale[:], grouped[:])
+            return code, scale
+
+        w3_code, w3_scale = quantize_weight(w3_raw, "w3")
+        w1_code, w1_scale = quantize_weight(w1_raw, "w1")
 
         out_rows = out.rearrange("(r p) n -> p r n", p=P)
         starts = [sum(CHUNKS[:c]) for c in range(len(CHUNKS))]
         last = len(CHUNKS) - 1
 
-        h_all = reuse.tile([P, S * PACK], BF16, name="h_all", offset=0, align_bytes=64)
+        h_all = keep.tile([P, S * PACK], BF16, name="h_all", align_bytes=64)
 
         def hidden(c):
             width = CHUNKS[c]
@@ -163,7 +158,12 @@ def tile_picked_lora_gelu_p_kernel(tc, x_words, x_scales, w1, w2, w3, offs, out)
                     nc.scalar.copy(result[:, r, :], accs[r][:])
                 else:
                     nc.vector.tensor_copy(result[:, r, :], accs[r][:])
-            nc.sync.dma_start(out_rows[:, :, starts[c] : starts[c] + width], result[:])
+            cols = slice(starts[c], starts[c] + width)
+            if c == last:
+                nc.sync.dma_start(out_rows[:, 0, cols], result[:, 0, :])
+                nc.scalar.dma_start(out_rows[:, 1, cols], result[:, 1, :])
+            else:
+                nc.sync.dma_start(out_rows[:, :, cols], result[:])
 
         made = [hidden(c) for c in range(len(CHUNKS))]
 
@@ -171,7 +171,7 @@ def tile_picked_lora_gelu_p_kernel(tc, x_words, x_scales, w1, w2, w3, offs, out)
             nc.vector.quantize_mx(code.bitcast(FP8X4), scale, made[c])
             return code, scale
 
-        early = reuse.tile([P, HALF], U32, name="h_early", offset=8192, align_bytes=64)
+        early = keep.tile([P, HALF], U32, name="h_early", tag="w1_raw", align_bytes=64)
         late = keep.tile([P, HALF], U32, name="h_late", align_bytes=64)
         s0 = keep.tile([P, 256], U8, name="s0", tag="even", align_bytes=64)
         s1 = keep.tile([P, 256], U8, name="s1", tag="odd", align_bytes=64)

@@ -19,49 +19,55 @@ PACK = 4
 HALF = S // 2
 UNIT = 128
 CHUNKS = (256, 256, 256, 128, 128)
-SCALAR_SHARE = 16
-FIRST = 896
+SCALAR_SHARE = 48
+FIRST = 1024
 
 
 def tile_picked_lora_gelu_p_kernel(tc, x_words, x_scales, w1, w2, w3, offs, out):
     nc = tc.nc
     with ExitStack() as ctx:
         keep = ctx.enter_context(tc.tile_pool(name="keep", bufs=1))
+        reuse = ctx.enter_context(tc.tile_pool(name="reuse", bufs=1))
         psum = ctx.enter_context(tc.psum_pool(name="psum", bufs=1))
 
         offsets = keep.tile([P, S // 16], U16, name="offsets")
         nc.sync.dma_start(offsets[:], offs)
 
-        scale_table = keep.tile([P, T], U8, name="scale_table", align_bytes=64)
-        nc.gpsimd.memset(scale_table[:, 0 : T // 2].bitcast(I32), 0)
-        nc.vector.memset(scale_table[:, T // 2 : T].bitcast(I32), 0)
+        scale_table = reuse.tile([P, T], U8, name="scale_table", offset=7168, align_bytes=64)
+        nc.vector.memset(scale_table[:].bitcast(I32), 0)
         word_table = keep.tile([P, T], I32, name="word_table", align_bytes=64)
         words = x_words[0].rearrange("p n t -> p (n t)").bitcast(I32)
         nc.sync.dma_start(word_table[:, 0:FIRST], words[:, 0:FIRST])
         nc.sync.dma_start(scale_table[0:P:8, :].bitcast(I32), x_scales[0].bitcast(I32))
+        w2_raw = keep.tile([P, PACK * H], F32, name="w2_raw")
+        nc.sync.dma_start(w2_raw[:], w2.rearrange("(p j) c -> p (j c)", j=PACK))
         nc.sync.dma_start(word_table[:, FIRST:T], words[:, FIRST:T])
 
         warm = keep.tile([P, 2], F32, name="warm")
         nc.vector.memset(warm[:, 0:1], 0.0)
         nc.scalar.activation(warm[:, 1:2], warm[:, 0:1], GELU)
 
-        w2_rows = w2.rearrange("(p j) c -> p j c", j=PACK)
-        w2_raw = []
-        for half in range(2):
-            raw = keep.tile([P, PACK, H // 2], F32, name=f"w2_raw{half}")
-            nc.sync.dma_start(raw[:], w2_rows[:, :, half * (H // 2) : (half + 1) * (H // 2)])
-            w2_raw.append(raw)
-        w3_raw = keep.tile([P, PACK * N], F32, name="w3_raw")
-        nc.sync.dma_start(w3_raw[:], w3.rearrange("(p j) c -> p (j c)", j=PACK))
-        w1_raw = keep.tile([P, PACK * N], F32, name="w1_raw", tag="w1_raw", align_bytes=64)
-        nc.sync.dma_start(w1_raw[:], w1.rearrange("(p j) c -> p (j c)", j=PACK))
 
         x_scale = keep.tile([P, S], U8, name="x_scale", align_bytes=64)
         nc.vector.memset(x_scale[:].bitcast(I32), 0)
         spread = keep.tile([P, S], U8, name="spread", align_bytes=64)
         nc.vector.tensor_copy(spread[:], scale_table[:].indirect(offsets[:]))
         for r in range(4):
-            nc.scalar.dma_start(x_scale[r:P:32, :].bitcast(I32), spread[8 * r : P : 32, :].bitcast(I32))
+            nc.sync.dma_start(x_scale[r:P:32, :].bitcast(I32), spread[8 * r : P : 32, :].bitcast(I32))
+        w3_raw = reuse.tile([P, PACK * N], F32, name="w3_raw", offset=4096, align_bytes=64)
+        nc.sync.dma_start(w3_raw[:], w3.rearrange("(p j) c -> p (j c)", j=PACK))
+        w1_raw = reuse.tile([P, PACK * N], F32, name="w1_raw", offset=10240, align_bytes=64)
+        nc.sync.dma_start(w1_raw[:], w1.rearrange("(p j) c -> p (j c)", j=PACK))
+        w2_bf = keep.tile([P, PACK * P * PACK], BF16, name="w2_bf", align_bytes=64)
+        dealt = w2_bf[:].rearrange("p (t m j) -> p m t j", t=PACK, j=PACK)
+        src = w2_raw[:].rearrange("p (j m t) -> p m t j", j=PACK, t=PACK)
+        nc.scalar.copy(dealt[:, 0:SCALAR_SHARE], src[:, 0:SCALAR_SHARE])
+        nc.vector.tensor_copy(dealt[:, SCALAR_SHARE:P], src[:, SCALAR_SHARE:P])
+        w2_all = keep.tile([P, H], U32, name="w2_all", align_bytes=64)
+        w2_planes = keep.tile([P, H], U8, name="w2_planes", align_bytes=64)
+        nc.vector.quantize_mx(w2_all[:].bitcast(FP8X4), w2_planes[:], w2_bf[:])
+        w2_code = [w2_all[:, t * P : (t + 1) * P] for t in range(PACK)]
+        w2_scale = [w2_planes[:, t * P : (t + 1) * P] for t in range(PACK)]
         x_code = []
 
         def gather_words(half, tag):
@@ -71,52 +77,35 @@ def tile_picked_lora_gelu_p_kernel(tc, x_words, x_scales, w1, w2, w3, offs, out)
             x_code.append(picked)
 
         gather_words(0, "first_words")
-        idle_bank = psum.tile([P, HALF], F32, name="idle_bank", tag="bank7")
-        for rep in range(4):
-            nc.tensor.matmul_mx(
-                idle_bank[:], lhsT=x_code[0][:, 0:P].bitcast(FP8X4), lhsT_scale=spread[:, 0:P],
-                rhs=x_code[0][:].bitcast(FP8X4), rhs_scale=spread[:, 0:HALF], start=True, stop=True,
-            )
         gather_words(1, "second_words")
 
         def tokens(start, width):
             half, at = divmod(start, HALF)
             return x_code[half][:, at : at + width].bitcast(FP8X4), x_scale[:, start : start + width]
 
-        M2 = P // 2
-        w2_bf = keep.tile([P, PACK * P * PACK], BF16, name="w2_bf", align_bytes=64)
-        dealt = w2_bf[:].rearrange("p (t m j) -> p m t j", t=PACK, j=PACK)
-        src = [raw[:].rearrange("p j (m t) -> p m t j", t=PACK) for raw in w2_raw]
-        nc.scalar.copy(dealt[:, 0:M2], src[0])
-        nc.vector.tensor_copy(dealt[:, M2 : P - SCALAR_SHARE], src[1][:, 0 : M2 - SCALAR_SHARE])
-        nc.scalar.copy(dealt[:, P - SCALAR_SHARE : P], src[1][:, M2 - SCALAR_SHARE : M2])
-        w2_code, w2_scale = [], []
-        for t in range(PACK):
-            code = keep.tile([P, P], U32, name=f"w2_code{t}", align_bytes=64)
-            scale = keep.tile([P, P], U8, name=f"w2_scale{t}", align_bytes=64)
-            nc.vector.quantize_mx(code[:].bitcast(FP8X4), scale[:], w2_bf[:, t * P * PACK : (t + 1) * P * PACK])
-            w2_code.append(code)
-            w2_scale.append(scale)
 
-        def quantize_weight(raw, name):
-            grouped = keep.tile([P, N * PACK], BF16, name=f"{name}_bf", align_bytes=64)
-            nc.vector.tensor_copy(
-                grouped[:].rearrange("p (c i j) -> p c j i", i=4, j=PACK),
-                raw[:].rearrange("p (j c i) -> p c j i", j=PACK, i=4),
-            )
-            code = keep.tile([P, N], U32, name=f"{name}_code", align_bytes=64)
-            scale = keep.tile([P, N], U8, name=f"{name}_scale", align_bytes=64)
-            nc.vector.quantize_mx(code[:].bitcast(FP8X4), scale[:], grouped[:])
-            return code, scale
-
-        w3_code, w3_scale = quantize_weight(w3_raw, "w3")
-        w1_code, w1_scale = quantize_weight(w1_raw, "w1")
+        w3_bf = keep.tile([P, N * PACK], BF16, name="w3_bf", align_bytes=64)
+        nc.scalar.copy(
+            w3_bf[:].rearrange("p (c i j) -> p c j i", i=4, j=PACK),
+            w3_raw[:].rearrange("p (j c i) -> p c j i", j=PACK, i=4),
+        )
+        w1_bf = keep.tile([P, N * PACK], BF16, name="w1_bf", align_bytes=64)
+        nc.vector.tensor_copy(
+            w1_bf[:].rearrange("p (c i j) -> p c j i", i=4, j=PACK),
+            w1_raw[:].rearrange("p (j c i) -> p c j i", j=PACK, i=4),
+        )
+        w3_code = reuse.tile([P, N], U32, name="w3_code", offset=10240 + 2048, align_bytes=64)
+        w3_scale = keep.tile([P, N], U8, name="w3_scale", align_bytes=64)
+        nc.vector.quantize_mx(w3_code[:].bitcast(FP8X4), w3_scale[:], w3_bf[:])
+        w1_code = keep.tile([P, N], U32, name="w1_code", align_bytes=64)
+        w1_scale = keep.tile([P, N], U8, name="w1_scale", align_bytes=64)
+        nc.vector.quantize_mx(w1_code[:].bitcast(FP8X4), w1_scale[:], w1_bf[:])
 
         out_rows = out.rearrange("(r p) n -> p r n", p=P)
         starts = [sum(CHUNKS[:c]) for c in range(len(CHUNKS))]
         last = len(CHUNKS) - 1
 
-        h_all = keep.tile([P, S * PACK], BF16, name="h_all", align_bytes=64)
+        h_all = reuse.tile([P, S * PACK], BF16, name="h_all", offset=0, align_bytes=64)
 
         def hidden(c):
             width = CHUNKS[c]
@@ -127,7 +116,7 @@ def tile_picked_lora_gelu_p_kernel(tc, x_words, x_scales, w1, w2, w3, offs, out)
                 code, scale = tokens(start, UNIT)
                 for t in range(PACK):
                     nc.tensor.matmul_mx(
-                        bank[:, t, :], lhsT=w2_code[t][:].bitcast(FP8X4), lhsT_scale=w2_scale[t][:],
+                        bank[:, t, :], lhsT=w2_code[t].bitcast(FP8X4), lhsT_scale=w2_scale[t],
                         rhs=code, rhs_scale=scale, start=True, stop=True,
                     )
                 nc.scalar.activation(
@@ -158,12 +147,7 @@ def tile_picked_lora_gelu_p_kernel(tc, x_words, x_scales, w1, w2, w3, offs, out)
                     nc.scalar.copy(result[:, r, :], accs[r][:])
                 else:
                     nc.vector.tensor_copy(result[:, r, :], accs[r][:])
-            cols = slice(starts[c], starts[c] + width)
-            if c == last:
-                nc.sync.dma_start(out_rows[:, 0, cols], result[:, 0, :])
-                nc.scalar.dma_start(out_rows[:, 1, cols], result[:, 1, :])
-            else:
-                nc.sync.dma_start(out_rows[:, :, cols], result[:])
+            nc.sync.dma_start(out_rows[:, :, starts[c] : starts[c] + width], result[:])
 
         made = [hidden(c) for c in range(len(CHUNKS))]
 
@@ -171,7 +155,7 @@ def tile_picked_lora_gelu_p_kernel(tc, x_words, x_scales, w1, w2, w3, offs, out)
             nc.vector.quantize_mx(code.bitcast(FP8X4), scale, made[c])
             return code, scale
 
-        early = keep.tile([P, HALF], U32, name="h_early", tag="w1_raw", align_bytes=64)
+        early = reuse.tile([P, HALF], U32, name="h_early", offset=10240, align_bytes=64)
         late = keep.tile([P, HALF], U32, name="h_late", align_bytes=64)
         s0 = keep.tile([P, 256], U8, name="s0", tag="even", align_bytes=64)
         s1 = keep.tile([P, 256], U8, name="s1", tag="odd", align_bytes=64)

@@ -16,11 +16,28 @@ GELU = mybir.ActivationFunctionType.Gelu_apprx_tanh
 
 P = 128
 PACK = 4
+LIST_ROWS = 16
+QUADRANT = 32
+SPREAD = 8
 HALF = S // 2
 UNIT = 128
+ROW_TILES = N // P
 CHUNKS = (256, 256, 256, 128, 128)
-SCALAR_SHARE = 48
-FIRST = 1024
+LONG_CHUNKS = 3
+SCALAR_CHUNK = 2
+HEAD_COLUMNS = 1024
+W2_SCALAR = 48
+
+HIDDEN_AT = 0
+W3_AT = 5632
+SCALE_TABLE_AT = 7168
+W1_AT = 10240
+EARLY_CODES_AT = W1_AT
+W3_CODES_AT = W1_AT + 2048
+
+
+def side_by_side(grouped, raw):
+    return grouped.rearrange("p (c i j) -> p c j i", i=4, j=PACK), raw.rearrange("p j (c i) -> p c j i", i=4)
 
 
 def tile_picked_lora_gelu_p_kernel(tc, x_words, x_scales, w1, w2, w3, offs, out):
@@ -30,144 +47,151 @@ def tile_picked_lora_gelu_p_kernel(tc, x_words, x_scales, w1, w2, w3, offs, out)
         reuse = ctx.enter_context(tc.tile_pool(name="reuse", bufs=1))
         psum = ctx.enter_context(tc.psum_pool(name="psum", bufs=1))
 
-        offsets = keep.tile([P, S // 16], U16, name="offsets")
+        offsets = keep.tile([P, S // LIST_ROWS], U16, name="offsets")
         nc.sync.dma_start(offsets[:], offs)
 
-        scale_table = reuse.tile([P, T], U8, name="scale_table", offset=7168, align_bytes=64)
+        scale_table = reuse.tile([P, T], U8, name="scale_table", offset=SCALE_TABLE_AT, align_bytes=64)
         nc.vector.memset(scale_table[:].bitcast(I32), 0)
         word_table = keep.tile([P, T], I32, name="word_table", align_bytes=64)
         words = x_words[0].rearrange("p n t -> p (n t)").bitcast(I32)
-        nc.sync.dma_start(word_table[:, 0:FIRST], words[:, 0:FIRST])
-        nc.sync.dma_start(scale_table[0:P:8, :].bitcast(I32), x_scales[0].bitcast(I32))
+        nc.sync.dma_start(word_table[:, 0:HEAD_COLUMNS], words[:, 0:HEAD_COLUMNS])
+        nc.sync.dma_start(scale_table[0:P:SPREAD, :].bitcast(I32), x_scales[0].bitcast(I32))
         w2_raw = keep.tile([P, PACK * H], F32, name="w2_raw")
         nc.sync.dma_start(w2_raw[:], w2.rearrange("(p j) c -> p (j c)", j=PACK))
-        nc.sync.dma_start(word_table[:, FIRST:T], words[:, FIRST:T])
+        nc.sync.dma_start(word_table[:, HEAD_COLUMNS:T], words[:, HEAD_COLUMNS:T])
 
         warm = keep.tile([P, 2], F32, name="warm")
         nc.vector.memset(warm[:, 0:1], 0.0)
         nc.scalar.activation(warm[:, 1:2], warm[:, 0:1], GELU)
 
-
         x_scale = keep.tile([P, S], U8, name="x_scale", align_bytes=64)
         nc.vector.memset(x_scale[:].bitcast(I32), 0)
-        spread = keep.tile([P, S], U8, name="spread", align_bytes=64)
-        nc.vector.tensor_copy(spread[:], scale_table[:].indirect(offsets[:]))
-        for r in range(4):
-            nc.sync.dma_start(x_scale[r:P:32, :].bitcast(I32), spread[8 * r : P : 32, :].bitcast(I32))
-        w3_raw = reuse.tile([P, PACK * N], F32, name="w3_raw", offset=4096, align_bytes=64)
-        nc.sync.dma_start(w3_raw[:], w3.rearrange("(p j) c -> p (j c)", j=PACK))
-        w1_raw = reuse.tile([P, PACK * N], F32, name="w1_raw", offset=10240, align_bytes=64)
+        spread_scale = keep.tile([P, S], U8, name="spread_scale", align_bytes=64)
+        nc.vector.tensor_copy(spread_scale[:], scale_table[:].indirect(offsets[:]))
+        for r in range(QUADRANT // SPREAD):
+            nc.sync.dma_start(
+                x_scale[r:P:QUADRANT, :].bitcast(I32), spread_scale[SPREAD * r : P : QUADRANT, :].bitcast(I32)
+            )
+
+        w3_rows = w3.rearrange("(p j) c -> p j c", j=PACK)
+        w3_raw = []
+        for r in range(ROW_TILES):
+            raw = reuse.tile([P, PACK, P], F32, name=f"w3_raw{r}", offset=W3_AT + 4 * PACK * P * r, align_bytes=64)
+            nc.sync.dma_start(raw[:], w3_rows[:, :, r * P : (r + 1) * P])
+            w3_raw.append(raw)
+        w1_raw = reuse.tile([P, PACK * N], F32, name="w1_raw", offset=W1_AT, align_bytes=64)
         nc.sync.dma_start(w1_raw[:], w1.rearrange("(p j) c -> p (j c)", j=PACK))
-        w2_bf = keep.tile([P, PACK * P * PACK], BF16, name="w2_bf", align_bytes=64)
+
+        w2_bf = keep.tile([P, PACK * H], BF16, name="w2_bf", align_bytes=64)
         dealt = w2_bf[:].rearrange("p (t m j) -> p m t j", t=PACK, j=PACK)
-        src = w2_raw[:].rearrange("p (j m t) -> p m t j", j=PACK, t=PACK)
-        nc.scalar.copy(dealt[:, 0:SCALAR_SHARE], src[:, 0:SCALAR_SHARE])
-        nc.vector.tensor_copy(dealt[:, SCALAR_SHARE:P], src[:, SCALAR_SHARE:P])
-        w2_all = keep.tile([P, H], U32, name="w2_all", align_bytes=64)
-        w2_planes = keep.tile([P, H], U8, name="w2_planes", align_bytes=64)
-        nc.vector.quantize_mx(w2_all[:].bitcast(FP8X4), w2_planes[:], w2_bf[:])
-        w2_code = [w2_all[:, t * P : (t + 1) * P] for t in range(PACK)]
-        w2_scale = [w2_planes[:, t * P : (t + 1) * P] for t in range(PACK)]
+        undealt = w2_raw[:].rearrange("p (j m t) -> p m t j", j=PACK, t=PACK)
+        nc.scalar.copy(dealt[:, 0:W2_SCALAR], undealt[:, 0:W2_SCALAR])
+        nc.vector.tensor_copy(dealt[:, W2_SCALAR:P], undealt[:, W2_SCALAR:P])
+        w2_code = keep.tile([P, H], U32, name="w2_code", align_bytes=64)
+        w2_scale = keep.tile([P, H], U8, name="w2_scale", align_bytes=64)
+        nc.vector.quantize_mx(w2_code[:].bitcast(FP8X4), w2_scale[:], w2_bf[:])
+
         x_code = []
-
-        def gather_words(half, tag):
-            picked = keep.tile([P, HALF], U32, name=f"x_code{half}", tag=tag, align_bytes=64)
-            cols = offsets[:, half * (HALF // 16) : (half + 1) * (HALF // 16)]
-            nc.vector.tensor_copy(picked[:], word_table[:].bitcast(U32).indirect(cols))
+        for half in range(S // HALF):
+            picked = keep.tile([P, HALF], U32, name=f"x_code{half}", align_bytes=64)
+            entries = offsets[:, half * (HALF // LIST_ROWS) : (half + 1) * (HALF // LIST_ROWS)]
+            nc.vector.tensor_copy(picked[:], word_table[:].bitcast(U32).indirect(entries))
             x_code.append(picked)
-
-        gather_words(0, "first_words")
-        gather_words(1, "second_words")
 
         def tokens(start, width):
             half, at = divmod(start, HALF)
             return x_code[half][:, at : at + width].bitcast(FP8X4), x_scale[:, start : start + width]
 
-
         w3_bf = keep.tile([P, N * PACK], BF16, name="w3_bf", align_bytes=64)
-        nc.scalar.copy(
-            w3_bf[:].rearrange("p (c i j) -> p c j i", i=4, j=PACK),
-            w3_raw[:].rearrange("p (j c i) -> p c j i", j=PACK, i=4),
-        )
+        for r in range(ROW_TILES):
+            nc.scalar.copy(*side_by_side(w3_bf[:, r * P * PACK : (r + 1) * P * PACK], w3_raw[r][:]))
         w1_bf = keep.tile([P, N * PACK], BF16, name="w1_bf", align_bytes=64)
-        nc.vector.tensor_copy(
-            w1_bf[:].rearrange("p (c i j) -> p c j i", i=4, j=PACK),
-            w1_raw[:].rearrange("p (j c i) -> p c j i", j=PACK, i=4),
-        )
-        w3_code = reuse.tile([P, N], U32, name="w3_code", offset=10240 + 2048, align_bytes=64)
+        nc.vector.tensor_copy(*side_by_side(w1_bf[:], w1_raw[:].rearrange("p (j c) -> p j c", j=PACK)))
+        w3_code = reuse.tile([P, N], U32, name="w3_code", offset=W3_CODES_AT, align_bytes=64)
         w3_scale = keep.tile([P, N], U8, name="w3_scale", align_bytes=64)
         nc.vector.quantize_mx(w3_code[:].bitcast(FP8X4), w3_scale[:], w3_bf[:])
         w1_code = keep.tile([P, N], U32, name="w1_code", align_bytes=64)
         w1_scale = keep.tile([P, N], U8, name="w1_scale", align_bytes=64)
         nc.vector.quantize_mx(w1_code[:].bitcast(FP8X4), w1_scale[:], w1_bf[:])
 
-        out_rows = out.rearrange("(r p) n -> p r n", p=P)
+        h_bf = reuse.tile([P, S * PACK], BF16, name="h_bf", offset=HIDDEN_AT, align_bytes=64)
+        for unit in range(S // UNIT):
+            bank = psum.tile([P, PACK, UNIT], F32, name="h_bank", tag=f"bank{unit}")
+            code, scale = tokens(unit * UNIT, UNIT)
+            for t in range(PACK):
+                nc.tensor.matmul_mx(
+                    bank[:, t, :],
+                    lhsT=w2_code[:, t * P : (t + 1) * P].bitcast(FP8X4),
+                    lhsT_scale=w2_scale[:, t * P : (t + 1) * P],
+                    rhs=code,
+                    rhs_scale=scale,
+                    start=True,
+                    stop=True,
+                )
+            nc.scalar.activation(
+                h_bf[:, unit * UNIT * PACK : (unit + 1) * UNIT * PACK].rearrange("p (n t) -> p n t", t=PACK),
+                bank[:].rearrange("p t n -> p n t"),
+                GELU,
+            )
+
         starts = [sum(CHUNKS[:c]) for c in range(len(CHUNKS))]
         last = len(CHUNKS) - 1
+        out_rows = out.rearrange("(r p) n -> p r n", p=P)
 
-        h_all = reuse.tile([P, S * PACK], BF16, name="h_all", offset=0, align_bytes=64)
+        def quantize_hidden(c, h_code, h_scale):
+            values = h_bf[:, starts[c] * PACK : (starts[c] + CHUNKS[c]) * PACK]
+            nc.vector.quantize_mx(h_code.bitcast(FP8X4), h_scale, values)
+            return h_code.bitcast(FP8X4), h_scale
 
-        def hidden(c):
+        def output(c, hidden):
             width = CHUNKS[c]
-            h_bf = h_all[:, starts[c] * PACK : (starts[c] + width) * PACK]
-            for u in range(width // UNIT):
-                start = starts[c] + u * UNIT
-                bank = psum.tile([P, PACK, UNIT], F32, name="h_bank", tag=f"bank{start // UNIT}")
-                code, scale = tokens(start, UNIT)
-                for t in range(PACK):
-                    nc.tensor.matmul_mx(
-                        bank[:, t, :], lhsT=w2_code[t].bitcast(FP8X4), lhsT_scale=w2_scale[t],
-                        rhs=code, rhs_scale=scale, start=True, stop=True,
-                    )
-                nc.scalar.activation(
-                    h_bf[:, u * UNIT * PACK : (u + 1) * UNIT * PACK].rearrange("p (n t) -> p n t", t=PACK),
-                    bank[:].rearrange("p t n -> p n t"),
-                    GELU,
-                )
-            return h_bf
-
-        def output(c, h_code, h_scale):
-            width = CHUNKS[c]
-            code, scale = tokens(starts[c], width)
-            accs = [psum.tile([P, width], F32, name=f"acc{r}", tag=f"bank{2 * (c % 3) + r}") for r in range(2)]
-            rows = [slice(r * P, (r + 1) * P) for r in range(2)]
-            for r in range(2):
+            pair = c % LONG_CHUNKS
+            accs = [
+                psum.tile([P, width], F32, name=f"acc{r}", tag=f"bank{ROW_TILES * pair + r}") for r in range(ROW_TILES)
+            ]
+            direct = (w1_code, w1_scale, tokens(starts[c], width))
+            adapter = (w3_code, w3_scale, hidden)
+            if c < LONG_CHUNKS:
+                passes = [(r, term, term is adapter) for r in range(ROW_TILES) for term in (adapter, direct)]
+            else:
+                passes = [(r, term, term is direct) for term in (direct, adapter) for r in range(ROW_TILES)]
+            for r, (w_code, w_scale, (rhs, rhs_scale)), opens in passes:
                 nc.tensor.matmul_mx(
-                    accs[r][:], lhsT=w1_code[:, rows[r]].bitcast(FP8X4), lhsT_scale=w1_scale[:, rows[r]],
-                    rhs=code, rhs_scale=scale, start=True, stop=False,
+                    accs[r][:],
+                    lhsT=w_code[:, r * P : (r + 1) * P].bitcast(FP8X4),
+                    lhsT_scale=w_scale[:, r * P : (r + 1) * P],
+                    rhs=rhs,
+                    rhs_scale=rhs_scale,
+                    start=opens,
+                    stop=not opens,
                 )
-            for r in range(2):
-                nc.tensor.matmul_mx(
-                    accs[r][:], lhsT=w3_code[:, rows[r]].bitcast(FP8X4), lhsT_scale=w3_scale[:, rows[r]],
-                    rhs=h_code.bitcast(FP8X4), rhs_scale=h_scale, start=False, stop=True,
-                )
-            result = keep.tile([P, 2, width], F32, name=f"result{c}")
-            for r in range(2):
-                if c == 2 or (c == last and r == 1):
+            result = keep.tile([P, ROW_TILES, width], F32, name=f"result{c}")
+            for r in range(ROW_TILES):
+                if c == SCALAR_CHUNK or (c == last and r == 1):
                     nc.scalar.copy(result[:, r, :], accs[r][:])
                 else:
                     nc.vector.tensor_copy(result[:, r, :], accs[r][:])
-            nc.sync.dma_start(out_rows[:, :, starts[c] : starts[c] + width], result[:])
+            cols = slice(starts[c], starts[c] + width)
+            if c == SCALAR_CHUNK:
+                for r in range(ROW_TILES):
+                    nc.sync.dma_start(out_rows[:, r, cols], result[:, r, :])
+            else:
+                nc.sync.dma_start(out_rows[:, :, cols], result[:])
 
-        made = [hidden(c) for c in range(len(CHUNKS))]
-
-        def quantize(c, code, scale):
-            nc.vector.quantize_mx(code.bitcast(FP8X4), scale, made[c])
-            return code, scale
-
-        early = reuse.tile([P, HALF], U32, name="h_early", offset=10240, align_bytes=64)
-        late = keep.tile([P, HALF], U32, name="h_late", align_bytes=64)
-        s0 = keep.tile([P, 256], U8, name="s0", tag="even", align_bytes=64)
-        s1 = keep.tile([P, 256], U8, name="s1", tag="odd", align_bytes=64)
-        q0 = quantize(0, early[:, 0:256], s0[:])
-        q1 = quantize(1, early[:, 256:512], s1[:])
-        output(0, *q0)
-        s2 = keep.tile([P, 256], U8, name="s2", tag="even", align_bytes=64)
-        q2 = quantize(2, late[:, 0:256], s2[:])
-        output(1, *q1)
-        s3 = keep.tile([P, 256], U8, name="s3", tag="odd", align_bytes=64)
-        q3 = quantize(3, late[:, 256:384], s3[:, 0:128])
-        q4 = quantize(4, late[:, 384:512], s3[:, 128:256])
-        output(2, *q2)
-        output(3, *q3)
-        output(4, *q4)
+        long, short = CHUNKS[0], CHUNKS[last]
+        early_code = reuse.tile([P, HALF], U32, name="early_code", offset=EARLY_CODES_AT, align_bytes=64)
+        late_code = keep.tile([P, HALF], U32, name="late_code", align_bytes=64)
+        plane0 = keep.tile([P, long], U8, name="plane0", tag="even", align_bytes=64)
+        plane1 = keep.tile([P, long], U8, name="plane1", tag="odd", align_bytes=64)
+        h0 = quantize_hidden(0, early_code[:, 0:long], plane0[:])
+        h1 = quantize_hidden(1, early_code[:, long:HALF], plane1[:])
+        output(0, h0)
+        plane2 = keep.tile([P, long], U8, name="plane2", tag="even", align_bytes=64)
+        h2 = quantize_hidden(2, late_code[:, 0:long], plane2[:])
+        output(1, h1)
+        plane34 = keep.tile([P, long], U8, name="plane34", tag="odd", align_bytes=64)
+        h3 = quantize_hidden(3, late_code[:, long : long + short], plane34[:, 0:short])
+        h4 = quantize_hidden(4, late_code[:, long + short : HALF], plane34[:, short:long])
+        output(2, h2)
+        output(3, h3)
+        output(4, h4)

@@ -22,18 +22,14 @@ SPREAD = 8
 HALF = S // 2
 UNIT = 128
 ROW_TILES = N // P
-CHUNKS = (256, 256, 256, 128, 128)
-LONG_CHUNKS = 3
-SCALAR_CHUNK = 2
-HEAD_COLUMNS = 1024
 W2_SCALAR = 48
+CHUNK = 256
+HEAD_COLUMNS = 1024
 
 HIDDEN_AT = 0
 W3_AT = 5632
 SCALE_TABLE_AT = 7168
 W1_AT = 10240
-EARLY_CODES_AT = W1_AT
-W3_CODES_AT = W1_AT + 2048
 
 
 def side_by_side(grouped, raw):
@@ -47,14 +43,13 @@ def tile_picked_lora_gelu_p_kernel(tc, x_words, x_scales, w1, w2, w3, offs, out)
         reuse = ctx.enter_context(tc.tile_pool(name="reuse", bufs=1))
         psum = ctx.enter_context(tc.psum_pool(name="psum", bufs=1))
 
-        offsets = keep.tile([P, S // LIST_ROWS], U16, name="offsets")
-        nc.sync.dma_start(offsets[:], offs)
-
         scale_table = reuse.tile([P, T], U8, name="scale_table", offset=SCALE_TABLE_AT, align_bytes=64)
         nc.vector.memset(scale_table[:].bitcast(I32), 0)
         word_table = keep.tile([P, T], I32, name="word_table", align_bytes=64)
         words = x_words[0].rearrange("p n t -> p (n t)").bitcast(I32)
         nc.sync.dma_start(word_table[:, 0:HEAD_COLUMNS], words[:, 0:HEAD_COLUMNS])
+        offsets = keep.tile([P, S // LIST_ROWS], U16, name="offsets")
+        nc.sync.dma_start(offsets[:], offs)
         nc.sync.dma_start(scale_table[0:P:SPREAD, :].bitcast(I32), x_scales[0].bitcast(I32))
         w2_raw = keep.tile([P, PACK * H], F32, name="w2_raw")
         nc.sync.dma_start(w2_raw[:], w2.rearrange("(p j) c -> p (j c)", j=PACK))
@@ -91,6 +86,18 @@ def tile_picked_lora_gelu_p_kernel(tc, x_words, x_scales, w1, w2, w3, offs, out)
         w2_scale = keep.tile([P, H], U8, name="w2_scale", align_bytes=64)
         nc.vector.quantize_mx(w2_code[:].bitcast(FP8X4), w2_scale[:], w2_bf[:])
 
+        idle = psum.tile([P, H], F32, name="idle", tag="bank7")
+        for scale in 3 * [w2_scale[:]] + 1 * [x_scale[:, 0:H]]:
+            nc.tensor.matmul_mx(
+                idle[:],
+                lhsT=w2_code[:, 0:P].bitcast(FP8X4),
+                lhsT_scale=w2_scale[:, 0:P],
+                rhs=w2_code[:].bitcast(FP8X4),
+                rhs_scale=scale,
+                start=True,
+                stop=True,
+            )
+
         x_code = []
         for half in range(S // HALF):
             picked = keep.tile([P, HALF], U32, name=f"x_code{half}", align_bytes=64)
@@ -102,21 +109,28 @@ def tile_picked_lora_gelu_p_kernel(tc, x_words, x_scales, w1, w2, w3, offs, out)
             half, at = divmod(start, HALF)
             return x_code[half][:, at : at + width].bitcast(FP8X4), x_scale[:, start : start + width]
 
+        def rounded(name, raw):
+            bf = keep.tile([P, N * PACK], BF16, name=f"{name}_bf", align_bytes=64)
+            nc.vector.tensor_copy(*side_by_side(bf[:], raw[:].rearrange("p (j c) -> p j c", j=PACK)))
+            return bf
+
+        def quantized(name, bf, code):
+            scale = keep.tile([P, N], U8, name=f"{name}_scale", align_bytes=64)
+            nc.vector.quantize_mx(code[:].bitcast(FP8X4), scale[:], bf[:])
+            return code, scale
+
         w3_bf = keep.tile([P, N * PACK], BF16, name="w3_bf", align_bytes=64)
         for r in range(ROW_TILES):
             nc.scalar.copy(*side_by_side(w3_bf[:, r * P * PACK : (r + 1) * P * PACK], w3_raw[r][:]))
-        w1_bf = keep.tile([P, N * PACK], BF16, name="w1_bf", align_bytes=64)
-        nc.vector.tensor_copy(*side_by_side(w1_bf[:], w1_raw[:].rearrange("p (j c) -> p j c", j=PACK)))
-        w3_code = reuse.tile([P, N], U32, name="w3_code", offset=W3_CODES_AT, align_bytes=64)
-        w3_scale = keep.tile([P, N], U8, name="w3_scale", align_bytes=64)
-        nc.vector.quantize_mx(w3_code[:].bitcast(FP8X4), w3_scale[:], w3_bf[:])
+        w3_code = keep.tile([P, N], U32, name="w3_code", align_bytes=64)
+        w3_code, w3_scale = quantized("w3", w3_bf, w3_code)
+        w1_bf = rounded("w1", w1_raw)
         w1_code = keep.tile([P, N], U32, name="w1_code", align_bytes=64)
-        w1_scale = keep.tile([P, N], U8, name="w1_scale", align_bytes=64)
-        nc.vector.quantize_mx(w1_code[:].bitcast(FP8X4), w1_scale[:], w1_bf[:])
+        w1_code, w1_scale = quantized("w1", w1_bf, w1_code)
 
         h_bf = reuse.tile([P, S * PACK], BF16, name="h_bf", offset=HIDDEN_AT, align_bytes=64)
         for unit in range(S // UNIT):
-            bank = psum.tile([P, PACK, UNIT], F32, name="h_bank", tag=f"bank{unit}")
+            bank = psum.tile([P, PACK, UNIT], F32, name="h_bank", tag=f"bank{unit % 6}")
             code, scale = tokens(unit * UNIT, UNIT)
             for t in range(PACK):
                 nc.tensor.matmul_mx(
@@ -129,69 +143,84 @@ def tile_picked_lora_gelu_p_kernel(tc, x_words, x_scales, w1, w2, w3, offs, out)
                     stop=True,
                 )
             nc.scalar.activation(
-                h_bf[:, unit * UNIT * PACK : (unit + 1) * UNIT * PACK].rearrange("p (n t) -> p n t", t=PACK),
-                bank[:].rearrange("p t n -> p n t"),
+                h_bf[:, unit * UNIT * PACK : (unit + 1) * UNIT * PACK].rearrange("p (c i t) -> p c t i", i=2, t=PACK),
+                bank[:].rearrange("p t (c i) -> p c t i", i=2),
                 GELU,
             )
 
-        starts = [sum(CHUNKS[:c]) for c in range(len(CHUNKS))]
-        last = len(CHUNKS) - 1
         out_rows = out.rearrange("(r p) n -> p r n", p=P)
+        h_code = reuse.tile([P, S], U32, name="h_code", offset=W1_AT, align_bytes=64)
 
-        def quantize_hidden(c, h_code, h_scale):
-            values = h_bf[:, starts[c] * PACK : (starts[c] + CHUNKS[c]) * PACK]
-            nc.vector.quantize_mx(h_code.bitcast(FP8X4), h_scale, values)
-            return h_code.bitcast(FP8X4), h_scale
+        def quantize_hidden(start, plane):
+            width = plane.shape[1]
+            code = h_code[:, start : start + width].bitcast(FP8X4)
+            nc.vector.quantize_mx(code, plane, h_bf[:, start * PACK : (start + width) * PACK])
+            return code, plane
 
-        def output(c, hidden):
-            width = CHUNKS[c]
-            pair = c % LONG_CHUNKS
-            accs = [
-                psum.tile([P, width], F32, name=f"acc{r}", tag=f"bank{ROW_TILES * pair + r}") for r in range(ROW_TILES)
-            ]
-            direct = (w1_code, w1_scale, tokens(starts[c], width))
-            adapter = (w3_code, w3_scale, hidden)
-            if c < LONG_CHUNKS:
-                passes = [(r, term, term is adapter) for r in range(ROW_TILES) for term in (adapter, direct)]
-            else:
-                passes = [(r, term, term is direct) for term in (direct, adapter) for r in range(ROW_TILES)]
-            for r, (w_code, w_scale, (rhs, rhs_scale)), opens in passes:
-                nc.tensor.matmul_mx(
-                    accs[r][:],
-                    lhsT=w_code[:, r * P : (r + 1) * P].bitcast(FP8X4),
-                    lhsT_scale=w_scale[:, r * P : (r + 1) * P],
-                    rhs=rhs,
-                    rhs_scale=rhs_scale,
-                    start=opens,
-                    stop=not opens,
-                )
-            result = keep.tile([P, ROW_TILES, width], F32, name=f"result{c}")
+        def product(acc, r, weights, moving, start=False, stop=False):
+            nc.tensor.matmul_mx(
+                acc,
+                lhsT=weights[0][:, r * P : (r + 1) * P].bitcast(FP8X4),
+                lhsT_scale=weights[1][:, r * P : (r + 1) * P],
+                rhs=moving[0],
+                rhs_scale=moving[1],
+                start=start,
+                stop=stop,
+            )
+
+        def store(c, result):
+            nc.sync.dma_start(out_rows[:, :, c * CHUNK : (c + 1) * CHUNK], result[:])
+
+        w1_mx, w3_mx = (w1_code, w1_scale), (w3_code, w3_scale)
+
+        def direct(accs, start, width, opens=(False, False), closes=(False, False)):
             for r in range(ROW_TILES):
-                if c == SCALAR_CHUNK or (c == last and r == 1):
-                    nc.scalar.copy(result[:, r, :], accs[r][:])
-                else:
-                    nc.vector.tensor_copy(result[:, r, :], accs[r][:])
-            cols = slice(starts[c], starts[c] + width)
-            if c == SCALAR_CHUNK:
-                for r in range(ROW_TILES):
-                    nc.sync.dma_start(out_rows[:, r, cols], result[:, r, :])
-            else:
-                nc.sync.dma_start(out_rows[:, :, cols], result[:])
+                product(accs[r], r, w1_mx, tokens(start, width), start=opens[r], stop=closes[r])
 
-        long, short = CHUNKS[0], CHUNKS[last]
-        early_code = reuse.tile([P, HALF], U32, name="early_code", offset=EARLY_CODES_AT, align_bytes=64)
-        late_code = keep.tile([P, HALF], U32, name="late_code", align_bytes=64)
-        plane0 = keep.tile([P, long], U8, name="plane0", tag="even", align_bytes=64)
-        plane1 = keep.tile([P, long], U8, name="plane1", tag="odd", align_bytes=64)
-        h0 = quantize_hidden(0, early_code[:, 0:long], plane0[:])
-        h1 = quantize_hidden(1, early_code[:, long:HALF], plane1[:])
-        output(0, h0)
-        plane2 = keep.tile([P, long], U8, name="plane2", tag="even", align_bytes=64)
-        h2 = quantize_hidden(2, late_code[:, 0:long], plane2[:])
-        output(1, h1)
-        plane34 = keep.tile([P, long], U8, name="plane34", tag="odd", align_bytes=64)
-        h3 = quantize_hidden(3, late_code[:, long : long + short], plane34[:, 0:short])
-        h4 = quantize_hidden(4, late_code[:, long + short : HALF], plane34[:, short:long])
-        output(2, h2)
-        output(3, h3)
-        output(4, h4)
+        def adapter(accs, hidden, opens=(False, False), closes=(False, False)):
+            for r in range(ROW_TILES):
+                product(accs[r], r, w3_mx, hidden, start=opens[r], stop=closes[r])
+
+        def rows(acc, cols=slice(None)):
+            return [acc[:, r, cols] for r in range(ROW_TILES)]
+
+        results = [keep.tile([P, ROW_TILES, CHUNK], F32, name=f"result{c}") for c in range(S // CHUNK)]
+        halves = [slice(0, UNIT), slice(UNIT, CHUNK)]
+        plane0 = keep.tile([P, CHUNK], U8, name="plane0", tag="even", align_bytes=64)
+        plane1 = keep.tile([P, CHUNK], U8, name="plane1", tag="odd", align_bytes=64)
+        h0 = quantize_hidden(0, plane0[:])
+        h1 = quantize_hidden(CHUNK, plane1[:])
+
+        acc0 = psum.tile([P, ROW_TILES, CHUNK], F32, name="acc0", tag="bank6")
+        direct(rows(acc0), 0, CHUNK, (True, False))
+        adapter(rows(acc0), h0, closes=(False, True))
+        nc.vector.tensor_copy(results[0][:], acc0[:])
+        store(0, results[0])
+
+        plane2 = keep.tile([P, CHUNK], U8, name="plane2", tag="even", align_bytes=64)
+        h2 = [quantize_hidden(2 * CHUNK + half.start, plane2[:, half]) for half in halves]
+        acc1 = psum.tile([P, ROW_TILES, CHUNK], F32, name="acc1", tag="bank7")
+        adapter(rows(acc1), h1, opens=(True, False))
+        direct(rows(acc1), CHUNK, CHUNK, closes=(False, True))
+        nc.vector.tensor_copy(results[1][:], acc1[:])
+        store(1, results[1])
+
+        plane3 = keep.tile([P, CHUNK], U8, name="plane3", tag="odd", align_bytes=64)
+        h3 = [quantize_hidden(3 * CHUNK + half.start, plane3[:, half]) for half in halves]
+        acc2 = psum.tile([P, ROW_TILES, CHUNK], F32, name="acc2", tag="bank6")
+        direct(rows(acc2), 2 * CHUNK, CHUNK, (True, False))
+        adapter(rows(acc2, halves[0]), h2[0])
+        adapter(rows(acc2, halves[1]), h2[1], closes=(False, True))
+        nc.scalar.copy(results[2][:], acc2[:])
+        store(2, results[2])
+
+        acc3 = psum.tile([P, ROW_TILES, UNIT], F32, name="acc3", tag="bank7")
+        direct(rows(acc3), 3 * CHUNK, UNIT, (True, False))
+        adapter(rows(acc3), h3[0], closes=(False, True))
+        nc.vector.tensor_copy(results[3][:, :, halves[0]], acc3[:])
+        last = [psum.tile([P, UNIT], F32, name=f"last{r}", tag=f"bank{2 + r}")[:] for r in range(ROW_TILES)]
+        direct(last, 3 * CHUNK + UNIT, UNIT, (True, True))
+        adapter(last, h3[1], closes=(True, True))
+        nc.scalar.copy(results[3][:, 0, halves[1]], last[0])
+        nc.vector.tensor_copy(results[3][:, 1, halves[1]], last[1])
+        store(3, results[3])

@@ -18,18 +18,24 @@ P = 128
 PACK = 4
 LIST_ROWS = 16
 QUADRANT = 32
-SPREAD = 8
+SCALE_ROWS = 16
 HALF = S // 2
 UNIT = 128
 ROW_TILES = N // P
 W2_SCALAR = 48
 CHUNK = 256
 HEAD_COLUMNS = 1024
+TAIL_COLUMNS = 512
+TABLE_ROW0 = 32
+TABLE_STEP = 4
+
+PIECES = (256, 256, 512)
 
 HIDDEN_AT = 0
-W3_AT = 5632
+W3_AT = (6144, 8192)
 SCALE_TABLE_AT = 7168
-W1_AT = 10240
+W1_AT = 11008
+LATER_CODE_AT = 14336
 
 
 def side_by_side(grouped, raw):
@@ -50,10 +56,10 @@ def tile_picked_lora_gelu_p_kernel(tc, x_words, x_scales, w1, w2, w3, offs, out)
         nc.sync.dma_start(word_table[:, 0:HEAD_COLUMNS], words[:, 0:HEAD_COLUMNS])
         offsets = keep.tile([P, S // LIST_ROWS], U16, name="offsets")
         nc.sync.dma_start(offsets[:], offs)
-        nc.sync.dma_start(scale_table[0:P:SPREAD, :].bitcast(I32), x_scales[0].bitcast(I32))
+        nc.sync.dma_start(scale_table[TABLE_ROW0 : TABLE_ROW0 + TABLE_STEP * SCALE_ROWS : TABLE_STEP, :].bitcast(I32), x_scales[0].bitcast(I32))
         w2_raw = keep.tile([P, PACK * H], F32, name="w2_raw")
         nc.sync.dma_start(w2_raw[:], w2.rearrange("(p j) c -> p (j c)", j=PACK))
-        nc.sync.dma_start(word_table[:, HEAD_COLUMNS:T], words[:, HEAD_COLUMNS:T])
+        nc.sync.dma_start(word_table[:, HEAD_COLUMNS : T - TAIL_COLUMNS], words[:, HEAD_COLUMNS : T - TAIL_COLUMNS])
 
         warm = keep.tile([P, 2], F32, name="warm")
         nc.vector.memset(warm[:, 0:1], 0.0)
@@ -63,15 +69,16 @@ def tile_picked_lora_gelu_p_kernel(tc, x_words, x_scales, w1, w2, w3, offs, out)
         nc.vector.memset(x_scale[:].bitcast(I32), 0)
         spread_scale = keep.tile([P, S], U8, name="spread_scale", align_bytes=64)
         nc.vector.tensor_copy(spread_scale[:], scale_table[:].indirect(offsets[:]))
-        for r in range(QUADRANT // SPREAD):
-            nc.sync.dma_start(
-                x_scale[r:P:QUADRANT, :].bitcast(I32), spread_scale[SPREAD * r : P : QUADRANT, :].bitcast(I32)
-            )
+        for r in range(PACK):
+            first = TABLE_ROW0 + TABLE_STEP * r
+            rows_r = slice(first, first + TABLE_STEP * PACK * 3 + 1, TABLE_STEP * PACK)
+            nc.sync.dma_start(x_scale[r:P:QUADRANT, :].bitcast(I32), spread_scale[rows_r, :].bitcast(I32))
+        nc.sync.dma_start(word_table[:, T - TAIL_COLUMNS : T], words[:, T - TAIL_COLUMNS : T])
 
         w3_rows = w3.rearrange("(p j) c -> p j c", j=PACK)
         w3_raw = []
         for r in range(ROW_TILES):
-            raw = reuse.tile([P, PACK, P], F32, name=f"w3_raw{r}", offset=W3_AT + 4 * PACK * P * r, align_bytes=64)
+            raw = reuse.tile([P, PACK, P], F32, name=f"w3_raw{r}", offset=W3_AT[r], align_bytes=64)
             nc.sync.dma_start(raw[:], w3_rows[:, :, r * P : (r + 1) * P])
             w3_raw.append(raw)
         w1_raw = reuse.tile([P, PACK * N], F32, name="w1_raw", offset=W1_AT, align_bytes=64)
@@ -87,49 +94,36 @@ def tile_picked_lora_gelu_p_kernel(tc, x_words, x_scales, w1, w2, w3, offs, out)
         nc.vector.quantize_mx(w2_code[:].bitcast(FP8X4), w2_scale[:], w2_bf[:])
 
         idle = psum.tile([P, H], F32, name="idle", tag="bank7")
-        for scale in 3 * [w2_scale[:]] + 1 * [x_scale[:, 0:H]]:
+        for width in (H, H // 2):
             nc.tensor.matmul_mx(
-                idle[:],
+                idle[:, 0:width],
                 lhsT=w2_code[:, 0:P].bitcast(FP8X4),
                 lhsT_scale=w2_scale[:, 0:P],
-                rhs=w2_code[:].bitcast(FP8X4),
-                rhs_scale=scale,
+                rhs=w2_code[:, 0:width].bitcast(FP8X4),
+                rhs_scale=x_scale[:, 0:width],
                 start=True,
                 stop=True,
             )
 
-        x_code = []
-        for half in range(S // HALF):
-            picked = keep.tile([P, HALF], U32, name=f"x_code{half}", align_bytes=64)
-            entries = offsets[:, half * (HALF // LIST_ROWS) : (half + 1) * (HALF // LIST_ROWS)]
-            nc.vector.tensor_copy(picked[:], word_table[:].bitcast(U32).indirect(entries))
-            x_code.append(picked)
+        starts = [sum(PIECES[:n]) for n in range(len(PIECES))]
+        x_code = [
+            keep.tile([P, PIECES[0]], U32, name="x_code0", align_bytes=64),
+            keep.tile([P, PIECES[1]], U32, name="x_code1", align_bytes=64),
+            keep.tile([P, PIECES[2]], U32, name="x_code2", align_bytes=64),
+        ]
+
+        def gather(n):
+            entries = offsets[:, starts[n] // LIST_ROWS : (starts[n] + PIECES[n]) // LIST_ROWS]
+            nc.vector.tensor_copy(x_code[n][:], word_table[:].bitcast(U32).indirect(entries))
 
         def tokens(start, width):
-            half, at = divmod(start, HALF)
-            return x_code[half][:, at : at + width].bitcast(FP8X4), x_scale[:, start : start + width]
-
-        def rounded(name, raw):
-            bf = keep.tile([P, N * PACK], BF16, name=f"{name}_bf", align_bytes=64)
-            nc.vector.tensor_copy(*side_by_side(bf[:], raw[:].rearrange("p (j c) -> p j c", j=PACK)))
-            return bf
-
-        def quantized(name, bf, code):
-            scale = keep.tile([P, N], U8, name=f"{name}_scale", align_bytes=64)
-            nc.vector.quantize_mx(code[:].bitcast(FP8X4), scale[:], bf[:])
-            return code, scale
-
-        w3_bf = keep.tile([P, N * PACK], BF16, name="w3_bf", align_bytes=64)
-        for r in range(ROW_TILES):
-            nc.scalar.copy(*side_by_side(w3_bf[:, r * P * PACK : (r + 1) * P * PACK], w3_raw[r][:]))
-        w3_code = keep.tile([P, N], U32, name="w3_code", align_bytes=64)
-        w3_code, w3_scale = quantized("w3", w3_bf, w3_code)
-        w1_bf = rounded("w1", w1_raw)
-        w1_code = keep.tile([P, N], U32, name="w1_code", align_bytes=64)
-        w1_code, w1_scale = quantized("w1", w1_bf, w1_code)
+            n = max(i for i in range(len(PIECES)) if starts[i] <= start)
+            at = start - starts[n]
+            return x_code[n][:, at : at + width].bitcast(FP8X4), x_scale[:, start : start + width]
 
         h_bf = reuse.tile([P, S * PACK], BF16, name="h_bf", offset=HIDDEN_AT, align_bytes=64)
-        for unit in range(S // UNIT):
+
+        def hidden_unit(unit):
             bank = psum.tile([P, PACK, UNIT], F32, name="h_bank", tag=f"bank{unit % 6}")
             code, scale = tokens(unit * UNIT, UNIT)
             for t in range(PACK):
@@ -148,12 +142,31 @@ def tile_picked_lora_gelu_p_kernel(tc, x_words, x_scales, w1, w2, w3, offs, out)
                 GELU,
             )
 
+        gather(0)
+        gather(1)
+        gather(2)
+        out_bf = keep.tile([P, 2 * N * PACK], BF16, name="out_bf", align_bytes=64)
+        nc.scalar.copy(*side_by_side(out_bf[:, 0 : P * PACK], w3_raw[0][:]))
+        for unit in range(S // UNIT):
+            hidden_unit(unit)
+        nc.gpsimd.tensor_scalar(
+            out_bf[:, P * PACK : N * PACK].rearrange("p (c j) -> p c j", j=PACK),
+            w3_raw[1][:].rearrange("p j c -> p c j"),
+            1.0,
+            0.0,
+            mybir.AluOpType.mult,
+            mybir.AluOpType.add,
+        )
+        nc.vector.tensor_copy(*side_by_side(out_bf[:, N * PACK :], w1_raw[:].rearrange("p (j c) -> p j c", j=PACK)))
+
         out_rows = out.rearrange("(r p) n -> p r n", p=P)
-        h_code = reuse.tile([P, S], U32, name="h_code", offset=W1_AT, align_bytes=64)
+        h_code = reuse.tile([P, S - CHUNK], U32, name="h_code", offset=LATER_CODE_AT, align_bytes=64)
+        first_code = keep.tile([P, CHUNK], U32, name="first_code", align_bytes=64)
 
         def quantize_hidden(start, plane):
             width = plane.shape[1]
-            code = h_code[:, start : start + width].bitcast(FP8X4)
+            words_at = first_code[:] if start == 0 else h_code[:, start - CHUNK : start - CHUNK + width]
+            code = words_at.bitcast(FP8X4)
             nc.vector.quantize_mx(code, plane, h_bf[:, start * PACK : (start + width) * PACK])
             return code, plane
 
@@ -171,7 +184,9 @@ def tile_picked_lora_gelu_p_kernel(tc, x_words, x_scales, w1, w2, w3, offs, out)
         def store(c, result):
             nc.sync.dma_start(out_rows[:, :, c * CHUNK : (c + 1) * CHUNK], result[:])
 
-        w1_mx, w3_mx = (w1_code, w1_scale), (w3_code, w3_scale)
+        out_code = keep.tile([P, 2 * N], U32, name="out_code", align_bytes=64)
+        out_scale = keep.tile([P, 2 * N], U8, name="out_scale", align_bytes=64)
+        w3_mx, w1_mx = (out_code[:, 0:N], out_scale[:, 0:N]), (out_code[:, N:], out_scale[:, N:])
 
         def direct(accs, start, width, opens=(False, False), closes=(False, False)):
             for r in range(ROW_TILES):
@@ -189,7 +204,7 @@ def tile_picked_lora_gelu_p_kernel(tc, x_words, x_scales, w1, w2, w3, offs, out)
         plane0 = keep.tile([P, CHUNK], U8, name="plane0", tag="even", align_bytes=64)
         plane1 = keep.tile([P, CHUNK], U8, name="plane1", tag="odd", align_bytes=64)
         h0 = quantize_hidden(0, plane0[:])
-        h1 = quantize_hidden(CHUNK, plane1[:])
+        nc.vector.quantize_mx(out_code[:].bitcast(FP8X4), out_scale[:], out_bf[:])
 
         acc0 = psum.tile([P, ROW_TILES, CHUNK], F32, name="acc0", tag="bank6")
         direct(rows(acc0), 0, CHUNK, (True, False))
@@ -197,8 +212,9 @@ def tile_picked_lora_gelu_p_kernel(tc, x_words, x_scales, w1, w2, w3, offs, out)
         nc.vector.tensor_copy(results[0][:], acc0[:])
         store(0, results[0])
 
+        h1 = quantize_hidden(CHUNK, plane1[:])
         plane2 = keep.tile([P, CHUNK], U8, name="plane2", tag="even", align_bytes=64)
-        h2 = [quantize_hidden(2 * CHUNK + half.start, plane2[:, half]) for half in halves]
+        h2 = quantize_hidden(2 * CHUNK, plane2[:])
         acc1 = psum.tile([P, ROW_TILES, CHUNK], F32, name="acc1", tag="bank7")
         adapter(rows(acc1), h1, opens=(True, False))
         direct(rows(acc1), CHUNK, CHUNK, closes=(False, True))
@@ -209,18 +225,14 @@ def tile_picked_lora_gelu_p_kernel(tc, x_words, x_scales, w1, w2, w3, offs, out)
         h3 = [quantize_hidden(3 * CHUNK + half.start, plane3[:, half]) for half in halves]
         acc2 = psum.tile([P, ROW_TILES, CHUNK], F32, name="acc2", tag="bank6")
         direct(rows(acc2), 2 * CHUNK, CHUNK, (True, False))
-        adapter(rows(acc2, halves[0]), h2[0])
-        adapter(rows(acc2, halves[1]), h2[1], closes=(False, True))
+        adapter(rows(acc2), h2, closes=(False, True))
         nc.scalar.copy(results[2][:], acc2[:])
         store(2, results[2])
 
-        acc3 = psum.tile([P, ROW_TILES, UNIT], F32, name="acc3", tag="bank7")
-        direct(rows(acc3), 3 * CHUNK, UNIT, (True, False))
-        adapter(rows(acc3), h3[0], closes=(False, True))
-        nc.vector.tensor_copy(results[3][:, :, halves[0]], acc3[:])
-        last = [psum.tile([P, UNIT], F32, name=f"last{r}", tag=f"bank{2 + r}")[:] for r in range(ROW_TILES)]
-        direct(last, 3 * CHUNK + UNIT, UNIT, (True, True))
-        adapter(last, h3[1], closes=(True, True))
-        nc.scalar.copy(results[3][:, 0, halves[1]], last[0])
-        nc.vector.tensor_copy(results[3][:, 1, halves[1]], last[1])
+        last = [psum.tile([P, CHUNK], F32, name=f"last{r}", tag=f"bank{2 + r}") for r in range(ROW_TILES)]
+        direct([acc[:] for acc in last], 3 * CHUNK, CHUNK, (True, True))
+        adapter([acc[:, halves[0]] for acc in last], h3[0])
+        adapter([acc[:, halves[1]] for acc in last], h3[1], closes=(True, True))
+        nc.scalar.copy(results[3][:, 0, :], last[0][:])
+        nc.vector.tensor_copy(results[3][:, 1, :], last[1][:])
         store(3, results[3])

@@ -22,7 +22,9 @@ SCALE_ROWS = 16
 HALF = S // 2
 UNIT = 128
 ROW_TILES = N // P
-W2_SCALAR = 48
+W2_SCALAR = 56
+WARM_UPS = 4
+WARM_UP_ROWS = 32
 CHUNK = 256
 HEAD_COLUMNS = 1024
 TAIL_COLUMNS = 512
@@ -94,13 +96,13 @@ def tile_picked_lora_gelu_p_kernel(tc, x_words, x_scales, w1, w2, w3, offs, out)
         nc.vector.quantize_mx(w2_code[:].bitcast(FP8X4), w2_scale[:], w2_bf[:])
 
         idle = psum.tile([P, H], F32, name="idle", tag="bank7")
-        for width in (H, H // 2):
+        for turn in range(WARM_UPS):
             nc.tensor.matmul_mx(
-                idle[:, 0:width],
-                lhsT=w2_code[:, 0:P].bitcast(FP8X4),
-                lhsT_scale=w2_scale[:, 0:P],
-                rhs=w2_code[:, 0:width].bitcast(FP8X4),
-                rhs_scale=x_scale[:, 0:width],
+                idle[0:WARM_UP_ROWS, :],
+                lhsT=w2_code[:, 0:WARM_UP_ROWS].bitcast(FP8X4),
+                lhsT_scale=w2_scale[:, 0:WARM_UP_ROWS],
+                rhs=w2_code[:].bitcast(FP8X4),
+                rhs_scale=w2_scale[:],
                 start=True,
                 stop=True,
             )

@@ -22,22 +22,21 @@ SCALE_ROWS = 16
 HALF = S // 2
 UNIT = 128
 ROW_TILES = N // P
-W2_SCALAR = 56
+W2_SCALAR = 72
 WARM_UPS = 4
 WARM_UP_ROWS = 32
 CHUNK = 256
-HEAD_COLUMNS = 1024
-TAIL_COLUMNS = 512
+VECTOR_CLEARS = 512
+W2_HEAD = 768
 TABLE_ROW0 = 32
 TABLE_STEP = 4
 
-PIECES = (256, 256, 512)
+PIECES = (256, 512, 256)
 
 HIDDEN_AT = 0
-W3_AT = (6144, 8192)
-SCALE_TABLE_AT = 7168
-W1_AT = 11008
-LATER_CODE_AT = 14336
+W3_FIRST_AT = 6144
+W1_LAST_AT = 8192
+FIRST_PIECE_AT = 10240
 
 
 def side_by_side(grouped, raw):
@@ -51,17 +50,19 @@ def tile_picked_lora_gelu_p_kernel(tc, x_words, x_scales, w1, w2, w3, offs, out)
         reuse = ctx.enter_context(tc.tile_pool(name="reuse", bufs=1))
         psum = ctx.enter_context(tc.psum_pool(name="psum", bufs=1))
 
-        scale_table = reuse.tile([P, T], U8, name="scale_table", offset=SCALE_TABLE_AT, align_bytes=64)
-        nc.vector.memset(scale_table[:].bitcast(I32), 0)
-        word_table = keep.tile([P, T], I32, name="word_table", align_bytes=64)
-        words = x_words[0].rearrange("p n t -> p (n t)").bitcast(I32)
-        nc.sync.dma_start(word_table[:, 0:HEAD_COLUMNS], words[:, 0:HEAD_COLUMNS])
+        scale_table = keep.tile([P, T], U8, name="scale_table", align_bytes=64)
+        table_words = scale_table[:].bitcast(I32)
+        nc.vector.memset(table_words[:, 0:VECTOR_CLEARS], 0)
+        nc.gpsimd.memset(table_words[:, VECTOR_CLEARS:], 0)
+        w2_raw = keep.tile([P, PACK * H], F32, name="w2_raw")
+        w2_rows = w2.rearrange("(p j) c -> p (j c)", j=PACK)
+        nc.sync.dma_start(w2_raw[:, 0:W2_HEAD], w2_rows[:, 0:W2_HEAD])
         offsets = keep.tile([P, S // LIST_ROWS], U16, name="offsets")
         nc.sync.dma_start(offsets[:], offs)
-        nc.sync.dma_start(scale_table[TABLE_ROW0 : TABLE_ROW0 + TABLE_STEP * SCALE_ROWS : TABLE_STEP, :].bitcast(I32), x_scales[0].bitcast(I32))
-        w2_raw = keep.tile([P, PACK * H], F32, name="w2_raw")
-        nc.sync.dma_start(w2_raw[:], w2.rearrange("(p j) c -> p (j c)", j=PACK))
-        nc.sync.dma_start(word_table[:, HEAD_COLUMNS : T - TAIL_COLUMNS], words[:, HEAD_COLUMNS : T - TAIL_COLUMNS])
+        nc.sync.dma_start(table_words[TABLE_ROW0 : TABLE_ROW0 + TABLE_STEP * SCALE_ROWS : TABLE_STEP, :], x_scales[0].bitcast(I32))
+        nc.sync.dma_start(w2_raw[:, W2_HEAD:], w2_rows[:, W2_HEAD:])
+        word_table = keep.tile([P, T], I32, name="word_table", align_bytes=64)
+        nc.sync.dma_start(word_table[:], x_words[0].rearrange("p n t -> p (n t)").bitcast(I32))
 
         warm = keep.tile([P, 2], F32, name="warm")
         nc.vector.memset(warm[:, 0:1], 0.0)
@@ -75,16 +76,17 @@ def tile_picked_lora_gelu_p_kernel(tc, x_words, x_scales, w1, w2, w3, offs, out)
             first = TABLE_ROW0 + TABLE_STEP * r
             rows_r = slice(first, first + TABLE_STEP * PACK * 3 + 1, TABLE_STEP * PACK)
             nc.sync.dma_start(x_scale[r:P:QUADRANT, :].bitcast(I32), spread_scale[rows_r, :].bitcast(I32))
-        nc.sync.dma_start(word_table[:, T - TAIL_COLUMNS : T], words[:, T - TAIL_COLUMNS : T])
 
-        w3_rows = w3.rearrange("(p j) c -> p j c", j=PACK)
-        w3_raw = []
-        for r in range(ROW_TILES):
-            raw = reuse.tile([P, PACK, P], F32, name=f"w3_raw{r}", offset=W3_AT[r], align_bytes=64)
-            nc.sync.dma_start(raw[:], w3_rows[:, :, r * P : (r + 1) * P])
-            w3_raw.append(raw)
-        w1_raw = reuse.tile([P, PACK * N], F32, name="w1_raw", offset=W1_AT, align_bytes=64)
-        nc.sync.dma_start(w1_raw[:], w1.rearrange("(p j) c -> p (j c)", j=PACK))
+        raw = {
+            ("w3", 0): reuse.tile([P, PACK, P], F32, name="w3_raw0", offset=W3_FIRST_AT, align_bytes=64),
+            ("w3", 1): keep.tile([P, PACK, P], F32, name="w3_raw1", align_bytes=64),
+            ("w1", 0): keep.tile([P, PACK, P], F32, name="w1_raw0", align_bytes=64),
+            ("w1", 1): reuse.tile([P, PACK, P], F32, name="w1_raw1", offset=W1_LAST_AT, align_bytes=64),
+        }
+        for name, weight in (("w3", w3), ("w1", w1)):
+            weight_rows = weight.rearrange("(p j) c -> p j c", j=PACK)
+            for r in range(ROW_TILES):
+                nc.sync.dma_start(raw[name, r][:], weight_rows[:, :, r * P : (r + 1) * P])
 
         w2_bf = keep.tile([P, PACK * H], BF16, name="w2_bf", align_bytes=64)
         dealt = w2_bf[:].rearrange("p (t m j) -> p m t j", t=PACK, j=PACK)
@@ -109,9 +111,9 @@ def tile_picked_lora_gelu_p_kernel(tc, x_words, x_scales, w1, w2, w3, offs, out)
 
         starts = [sum(PIECES[:n]) for n in range(len(PIECES))]
         x_code = [
-            keep.tile([P, PIECES[0]], U32, name="x_code0", align_bytes=64),
+            reuse.tile([P, PIECES[0]], U32, name="x_code0", offset=FIRST_PIECE_AT, align_bytes=64),
             keep.tile([P, PIECES[1]], U32, name="x_code1", align_bytes=64),
-            keep.tile([P, PIECES[2]], U32, name="x_code2", align_bytes=64),
+            reuse.tile([P, PIECES[2]], U32, name="x_code2", offset=W1_LAST_AT + 4 * CHUNK, align_bytes=64),
         ]
 
         def gather(n):
@@ -146,29 +148,45 @@ def tile_picked_lora_gelu_p_kernel(tc, x_words, x_scales, w1, w2, w3, offs, out)
 
         gather(0)
         gather(1)
-        gather(2)
-        out_bf = keep.tile([P, 2 * N * PACK], BF16, name="out_bf", align_bytes=64)
-        nc.scalar.copy(*side_by_side(out_bf[:, 0 : P * PACK], w3_raw[0][:]))
-        for unit in range(S // UNIT):
+        w3_bf = keep.tile([P, N * PACK], BF16, name="w3_bf", align_bytes=64)
+        w1_bf = keep.tile([P, N * PACK], BF16, name="w1_bf", align_bytes=64)
+
+        def round_on_gpsimd(grouped, rows_f32):
+            nc.gpsimd.tensor_scalar(
+                grouped.rearrange("p (c j) -> p c j", j=PACK),
+                rows_f32.rearrange("p j c -> p c j"),
+                1.0,
+                0.0,
+                mybir.AluOpType.mult,
+                mybir.AluOpType.add,
+            )
+
+        def quantized(name, bf):
+            code = keep.tile([P, N], U32, name=f"{name}_code", align_bytes=64)
+            scale = keep.tile([P, N], U8, name=f"{name}_scale", align_bytes=64)
+            nc.vector.quantize_mx(code[:].bitcast(FP8X4), scale[:], bf[:])
+            return code, scale
+
+        nc.scalar.copy(*side_by_side(w3_bf[:, 0 : P * PACK], raw["w3", 0][:]))
+        for unit in range(starts[2] // UNIT):
             hidden_unit(unit)
-        nc.gpsimd.tensor_scalar(
-            out_bf[:, P * PACK : N * PACK].rearrange("p (c j) -> p c j", j=PACK),
-            w3_raw[1][:].rearrange("p j c -> p c j"),
-            1.0,
-            0.0,
-            mybir.AluOpType.mult,
-            mybir.AluOpType.add,
-        )
-        nc.vector.tensor_copy(*side_by_side(out_bf[:, N * PACK :], w1_raw[:].rearrange("p (j c) -> p j c", j=PACK)))
+        round_on_gpsimd(w3_bf[:, P * PACK :], raw["w3", 1][:])
+        round_on_gpsimd(w1_bf[:, 0 : P * PACK], raw["w1", 0][:])
+        w3_mx = quantized("w3", w3_bf)
+        nc.vector.tensor_copy(*side_by_side(w1_bf[:, P * PACK :], raw["w1", 1][:]))
 
         out_rows = out.rearrange("(r p) n -> p r n", p=P)
-        h_code = reuse.tile([P, S - CHUNK], U32, name="h_code", offset=LATER_CODE_AT, align_bytes=64)
-        first_code = keep.tile([P, CHUNK], U32, name="first_code", align_bytes=64)
+        h_code = [
+            keep.tile([P, CHUNK], U32, name="h_code0", align_bytes=64),
+            reuse.tile([P, CHUNK], U32, name="h_code1", offset=W1_LAST_AT, align_bytes=64),
+            reuse.tile([P, CHUNK], U32, name="h_code2", offset=FIRST_PIECE_AT, align_bytes=64),
+            keep.tile([P, CHUNK], U32, name="h_code3", align_bytes=64),
+        ]
 
         def quantize_hidden(start, plane):
             width = plane.shape[1]
-            words_at = first_code[:] if start == 0 else h_code[:, start - CHUNK : start - CHUNK + width]
-            code = words_at.bitcast(FP8X4)
+            c, at = divmod(start, CHUNK)
+            code = h_code[c][:, at : at + width].bitcast(FP8X4)
             nc.vector.quantize_mx(code, plane, h_bf[:, start * PACK : (start + width) * PACK])
             return code, plane
 
@@ -186,10 +204,6 @@ def tile_picked_lora_gelu_p_kernel(tc, x_words, x_scales, w1, w2, w3, offs, out)
         def store(c, result):
             nc.sync.dma_start(out_rows[:, :, c * CHUNK : (c + 1) * CHUNK], result[:])
 
-        out_code = keep.tile([P, 2 * N], U32, name="out_code", align_bytes=64)
-        out_scale = keep.tile([P, 2 * N], U8, name="out_scale", align_bytes=64)
-        w3_mx, w1_mx = (out_code[:, 0:N], out_scale[:, 0:N]), (out_code[:, N:], out_scale[:, N:])
-
         def direct(accs, start, width, opens=(False, False), closes=(False, False)):
             for r in range(ROW_TILES):
                 product(accs[r], r, w1_mx, tokens(start, width), start=opens[r], stop=closes[r])
@@ -203,23 +217,26 @@ def tile_picked_lora_gelu_p_kernel(tc, x_words, x_scales, w1, w2, w3, offs, out)
 
         results = [keep.tile([P, ROW_TILES, CHUNK], F32, name=f"result{c}") for c in range(S // CHUNK)]
         halves = [slice(0, UNIT), slice(UNIT, CHUNK)]
-        plane0 = keep.tile([P, CHUNK], U8, name="plane0", tag="even", align_bytes=64)
+        plane0 = keep.tile([P, CHUNK], U8, name="plane0", align_bytes=64)
         plane1 = keep.tile([P, CHUNK], U8, name="plane1", tag="odd", align_bytes=64)
         h0 = quantize_hidden(0, plane0[:])
-        nc.vector.quantize_mx(out_code[:].bitcast(FP8X4), out_scale[:], out_bf[:])
+        w1_mx = quantized("w1", w1_bf)
+        gather(2)
+        h1 = quantize_hidden(CHUNK, plane1[:])
 
         acc0 = psum.tile([P, ROW_TILES, CHUNK], F32, name="acc0", tag="bank6")
-        direct(rows(acc0), 0, CHUNK, (True, False))
-        adapter(rows(acc0), h0, closes=(False, True))
+        adapter(rows(acc0), h0, opens=(True, False))
+        direct(rows(acc0), 0, CHUNK, closes=(False, True))
+        acc1 = psum.tile([P, ROW_TILES, CHUNK], F32, name="acc1", tag="bank7")
+        direct(rows(acc1), CHUNK, CHUNK, (True, False))
+        hidden_unit(6)
+        adapter(rows(acc1), h1, closes=(False, True))
+        hidden_unit(7)
         nc.vector.tensor_copy(results[0][:], acc0[:])
         store(0, results[0])
 
-        h1 = quantize_hidden(CHUNK, plane1[:])
-        plane2 = keep.tile([P, CHUNK], U8, name="plane2", tag="even", align_bytes=64)
+        plane2 = keep.tile([P, CHUNK], U8, name="plane2", align_bytes=64)
         h2 = quantize_hidden(2 * CHUNK, plane2[:])
-        acc1 = psum.tile([P, ROW_TILES, CHUNK], F32, name="acc1", tag="bank7")
-        adapter(rows(acc1), h1, opens=(True, False))
-        direct(rows(acc1), CHUNK, CHUNK, closes=(False, True))
         nc.vector.tensor_copy(results[1][:], acc1[:])
         store(1, results[1])
 

@@ -26,7 +26,6 @@ W2_SCALAR = 72
 WARM_UPS = 4
 WARM_UP_ROWS = 32
 CHUNK = 256
-VECTOR_CLEARS = 512
 W2_HEAD = 768
 TABLE_ROW0 = 32
 TABLE_STEP = 4
@@ -35,8 +34,8 @@ PIECES = (256, 512, 256)
 
 HIDDEN_AT = 0
 W3_FIRST_AT = 6144
-W1_LAST_AT = 8192
-FIRST_PIECE_AT = 10240
+W1_AT = 8192
+FIRST_PIECE_AT = 12288
 
 
 def side_by_side(grouped, raw):
@@ -52,8 +51,7 @@ def tile_picked_lora_gelu_p_kernel(tc, x_words, x_scales, w1, w2, w3, offs, out)
 
         scale_table = keep.tile([P, T], U8, name="scale_table", align_bytes=64)
         table_words = scale_table[:].bitcast(I32)
-        nc.vector.memset(table_words[:, 0:VECTOR_CLEARS], 0)
-        nc.gpsimd.memset(table_words[:, VECTOR_CLEARS:], 0)
+        nc.vector.memset(table_words, 0)
         w2_raw = keep.tile([P, PACK * H], F32, name="w2_raw")
         w2_rows = w2.rearrange("(p j) c -> p (j c)", j=PACK)
         nc.sync.dma_start(w2_raw[:, 0:W2_HEAD], w2_rows[:, 0:W2_HEAD])
@@ -77,16 +75,15 @@ def tile_picked_lora_gelu_p_kernel(tc, x_words, x_scales, w1, w2, w3, offs, out)
             rows_r = slice(first, first + TABLE_STEP * PACK * 3 + 1, TABLE_STEP * PACK)
             nc.sync.dma_start(x_scale[r:P:QUADRANT, :].bitcast(I32), spread_scale[rows_r, :].bitcast(I32))
 
-        raw = {
-            ("w3", 0): reuse.tile([P, PACK, P], F32, name="w3_raw0", offset=W3_FIRST_AT, align_bytes=64),
-            ("w3", 1): keep.tile([P, PACK, P], F32, name="w3_raw1", align_bytes=64),
-            ("w1", 0): keep.tile([P, PACK, P], F32, name="w1_raw0", align_bytes=64),
-            ("w1", 1): reuse.tile([P, PACK, P], F32, name="w1_raw1", offset=W1_LAST_AT, align_bytes=64),
-        }
-        for name, weight in (("w3", w3), ("w1", w1)):
-            weight_rows = weight.rearrange("(p j) c -> p j c", j=PACK)
-            for r in range(ROW_TILES):
-                nc.sync.dma_start(raw[name, r][:], weight_rows[:, :, r * P : (r + 1) * P])
+        w3_rows = w3.rearrange("(p j) c -> p j c", j=PACK)
+        w3_raw = [
+            reuse.tile([P, PACK, P], F32, name="w3_raw0", offset=W3_FIRST_AT, align_bytes=64),
+            keep.tile([P, PACK, P], F32, name="w3_raw1", align_bytes=64),
+        ]
+        for r in range(ROW_TILES):
+            nc.sync.dma_start(w3_raw[r][:], w3_rows[:, :, r * P : (r + 1) * P])
+        w1_raw = reuse.tile([P, PACK * N], F32, name="w1_raw", offset=W1_AT, align_bytes=64)
+        nc.sync.dma_start(w1_raw[:], w1.rearrange("(p j) c -> p (j c)", j=PACK))
 
         w2_bf = keep.tile([P, PACK * H], BF16, name="w2_bf", align_bytes=64)
         dealt = w2_bf[:].rearrange("p (t m j) -> p m t j", t=PACK, j=PACK)
@@ -113,7 +110,7 @@ def tile_picked_lora_gelu_p_kernel(tc, x_words, x_scales, w1, w2, w3, offs, out)
         x_code = [
             reuse.tile([P, PIECES[0]], U32, name="x_code0", offset=FIRST_PIECE_AT, align_bytes=64),
             keep.tile([P, PIECES[1]], U32, name="x_code1", align_bytes=64),
-            reuse.tile([P, PIECES[2]], U32, name="x_code2", offset=W1_LAST_AT + 4 * CHUNK, align_bytes=64),
+            reuse.tile([P, PIECES[2]], U32, name="x_code2", offset=W1_AT + 4 * CHUNK, align_bytes=64),
         ]
 
         def gather(n):
@@ -148,37 +145,17 @@ def tile_picked_lora_gelu_p_kernel(tc, x_words, x_scales, w1, w2, w3, offs, out)
 
         gather(0)
         gather(1)
-        w3_bf = keep.tile([P, N * PACK], BF16, name="w3_bf", align_bytes=64)
-        w1_bf = keep.tile([P, N * PACK], BF16, name="w1_bf", align_bytes=64)
-
-        def round_on_gpsimd(grouped, rows_f32):
-            nc.gpsimd.tensor_scalar(
-                grouped.rearrange("p (c j) -> p c j", j=PACK),
-                rows_f32.rearrange("p j c -> p c j"),
-                1.0,
-                0.0,
-                mybir.AluOpType.mult,
-                mybir.AluOpType.add,
-            )
-
-        def quantized(name, bf):
-            code = keep.tile([P, N], U32, name=f"{name}_code", align_bytes=64)
-            scale = keep.tile([P, N], U8, name=f"{name}_scale", align_bytes=64)
-            nc.vector.quantize_mx(code[:].bitcast(FP8X4), scale[:], bf[:])
-            return code, scale
-
-        nc.scalar.copy(*side_by_side(w3_bf[:, 0 : P * PACK], raw["w3", 0][:]))
+        out_bf = keep.tile([P, 2 * N * PACK], BF16, name="out_bf", align_bytes=64)
+        nc.scalar.copy(*side_by_side(out_bf[:, 0 : P * PACK], w3_raw[0][:]))
         for unit in range(starts[2] // UNIT):
             hidden_unit(unit)
-        round_on_gpsimd(w3_bf[:, P * PACK :], raw["w3", 1][:])
-        round_on_gpsimd(w1_bf[:, 0 : P * PACK], raw["w1", 0][:])
-        w3_mx = quantized("w3", w3_bf)
-        nc.vector.tensor_copy(*side_by_side(w1_bf[:, P * PACK :], raw["w1", 1][:]))
+        nc.vector.tensor_copy(*side_by_side(out_bf[:, P * PACK : N * PACK], w3_raw[1][:]))
+        nc.vector.tensor_copy(*side_by_side(out_bf[:, N * PACK :], w1_raw[:].rearrange("p (j c) -> p j c", j=PACK)))
 
         out_rows = out.rearrange("(r p) n -> p r n", p=P)
         h_code = [
             keep.tile([P, CHUNK], U32, name="h_code0", align_bytes=64),
-            reuse.tile([P, CHUNK], U32, name="h_code1", offset=W1_LAST_AT, align_bytes=64),
+            reuse.tile([P, CHUNK], U32, name="h_code1", offset=W1_AT, align_bytes=64),
             reuse.tile([P, CHUNK], U32, name="h_code2", offset=FIRST_PIECE_AT, align_bytes=64),
             keep.tile([P, CHUNK], U32, name="h_code3", align_bytes=64),
         ]
@@ -220,7 +197,10 @@ def tile_picked_lora_gelu_p_kernel(tc, x_words, x_scales, w1, w2, w3, offs, out)
         plane0 = keep.tile([P, CHUNK], U8, name="plane0", align_bytes=64)
         plane1 = keep.tile([P, CHUNK], U8, name="plane1", tag="odd", align_bytes=64)
         h0 = quantize_hidden(0, plane0[:])
-        w1_mx = quantized("w1", w1_bf)
+        out_code = keep.tile([P, 2 * N], U32, name="out_code", align_bytes=64)
+        out_scale = keep.tile([P, 2 * N], U8, name="out_scale", align_bytes=64)
+        nc.vector.quantize_mx(out_code[:].bitcast(FP8X4), out_scale[:], out_bf[:])
+        w3_mx, w1_mx = (out_code[:, 0:N], out_scale[:, 0:N]), (out_code[:, N:], out_scale[:, N:])
         gather(2)
         h1 = quantize_hidden(CHUNK, plane1[:])
 

@@ -30,11 +30,13 @@ W2_HEAD = 768
 TABLE_ROW0 = 32
 TABLE_STEP = 4
 
-PIECES = (256, 512, 256)
+PIECES = (256, 256, 512)
 
 HIDDEN_AT = 0
 W3_FIRST_AT = 6144
-W1_AT = 8192
+W3_LAST_AT = 9216
+OUT_CODE_AT = 8256
+SECOND_CODE_AT = 10304
 FIRST_PIECE_AT = 12288
 
 
@@ -78,12 +80,12 @@ def tile_picked_lora_gelu_p_kernel(tc, x_words, x_scales, w1, w2, w3, offs, out)
         w3_rows = w3.rearrange("(p j) c -> p j c", j=PACK)
         w3_raw = [
             reuse.tile([P, PACK, P], F32, name="w3_raw0", offset=W3_FIRST_AT, align_bytes=64),
-            keep.tile([P, PACK, P], F32, name="w3_raw1", align_bytes=64),
+            reuse.tile([P, PACK, P], F32, name="w3_raw1", offset=W3_LAST_AT, align_bytes=64),
         ]
-        for r in range(ROW_TILES):
-            nc.sync.dma_start(w3_raw[r][:], w3_rows[:, :, r * P : (r + 1) * P])
-        w1_raw = reuse.tile([P, PACK * N], F32, name="w1_raw", offset=W1_AT, align_bytes=64)
+        w1_raw = keep.tile([P, PACK * N], F32, name="w1_raw", align_bytes=64)
+        nc.sync.dma_start(w3_raw[0][:], w3_rows[:, :, 0:P])
         nc.sync.dma_start(w1_raw[:], w1.rearrange("(p j) c -> p (j c)", j=PACK))
+        nc.sync.dma_start(w3_raw[1][:], w3_rows[:, :, P:N])
 
         w2_bf = keep.tile([P, PACK * H], BF16, name="w2_bf", align_bytes=64)
         dealt = w2_bf[:].rearrange("p (t m j) -> p m t j", t=PACK, j=PACK)
@@ -110,7 +112,7 @@ def tile_picked_lora_gelu_p_kernel(tc, x_words, x_scales, w1, w2, w3, offs, out)
         x_code = [
             reuse.tile([P, PIECES[0]], U32, name="x_code0", offset=FIRST_PIECE_AT, align_bytes=64),
             keep.tile([P, PIECES[1]], U32, name="x_code1", align_bytes=64),
-            reuse.tile([P, PIECES[2]], U32, name="x_code2", offset=W1_AT + 4 * CHUNK, align_bytes=64),
+            keep.tile([P, PIECES[2]], U32, name="x_code2", align_bytes=64),
         ]
 
         def gather(n):
@@ -145,19 +147,23 @@ def tile_picked_lora_gelu_p_kernel(tc, x_words, x_scales, w1, w2, w3, offs, out)
 
         gather(0)
         gather(1)
-        out_bf = keep.tile([P, 2 * N * PACK], BF16, name="out_bf", align_bytes=64)
-        nc.scalar.copy(*side_by_side(out_bf[:, 0 : P * PACK], w3_raw[0][:]))
-        for unit in range(starts[2] // UNIT):
+        gather(2)
+        out_bf = keep.tile([P, ROW_TILES, 2, P * PACK], BF16, name="out_bf", align_bytes=64)
+        nc.scalar.copy(*side_by_side(out_bf[:, 0, 0, :], w3_raw[0][:]))
+        for unit in range(S // UNIT):
             hidden_unit(unit)
-        nc.vector.tensor_copy(*side_by_side(out_bf[:, P * PACK : N * PACK], w3_raw[1][:]))
-        nc.vector.tensor_copy(*side_by_side(out_bf[:, N * PACK :], w1_raw[:].rearrange("p (j c) -> p j c", j=PACK)))
+        nc.vector.tensor_copy(
+            out_bf[:, :, 1, :].rearrange("p r (c i j) -> p r c j i", i=4, j=PACK),
+            w1_raw[:].rearrange("p (j r c i) -> p r c j i", j=PACK, r=ROW_TILES, i=4),
+        )
+        nc.vector.tensor_copy(*side_by_side(out_bf[:, 1, 0, :], w3_raw[1][:]))
 
         out_rows = out.rearrange("(r p) n -> p r n", p=P)
         h_code = [
             keep.tile([P, CHUNK], U32, name="h_code0", align_bytes=64),
-            reuse.tile([P, CHUNK], U32, name="h_code1", offset=W1_AT, align_bytes=64),
-            reuse.tile([P, CHUNK], U32, name="h_code2", offset=FIRST_PIECE_AT, align_bytes=64),
-            keep.tile([P, CHUNK], U32, name="h_code3", align_bytes=64),
+            reuse.tile([P, CHUNK], U32, name="h_code1", offset=SECOND_CODE_AT, align_bytes=64),
+            keep.tile([P, CHUNK], U32, name="h_code2", align_bytes=64),
+            reuse.tile([P, CHUNK], U32, name="h_code3", offset=FIRST_PIECE_AT, align_bytes=64),
         ]
 
         def quantize_hidden(start, plane):
@@ -170,8 +176,8 @@ def tile_picked_lora_gelu_p_kernel(tc, x_words, x_scales, w1, w2, w3, offs, out)
         def product(acc, r, weights, moving, start=False, stop=False):
             nc.tensor.matmul_mx(
                 acc,
-                lhsT=weights[0][:, r * P : (r + 1) * P].bitcast(FP8X4),
-                lhsT_scale=weights[1][:, r * P : (r + 1) * P],
+                lhsT=out_code[r][:, weights].bitcast(FP8X4),
+                lhsT_scale=out_scale[:, r, weights],
                 rhs=moving[0],
                 rhs_scale=moving[1],
                 start=start,
@@ -192,46 +198,54 @@ def tile_picked_lora_gelu_p_kernel(tc, x_words, x_scales, w1, w2, w3, offs, out)
         def rows(acc, cols=slice(None)):
             return [acc[:, r, cols] for r in range(ROW_TILES)]
 
-        results = [keep.tile([P, ROW_TILES, CHUNK], F32, name=f"result{c}") for c in range(S // CHUNK)]
+        results = [keep.tile([P, ROW_TILES, CHUNK], F32, name=f"result{c}") for c in (0, 1)]
+        results.append(reuse.tile([P, ROW_TILES, CHUNK], F32, name="result2", offset=HIDDEN_AT, align_bytes=64))
+        results.append(keep.tile([P, ROW_TILES, CHUNK], F32, name="result3"))
         halves = [slice(0, UNIT), slice(UNIT, CHUNK)]
-        plane0 = keep.tile([P, CHUNK], U8, name="plane0", align_bytes=64)
-        plane1 = keep.tile([P, CHUNK], U8, name="plane1", tag="odd", align_bytes=64)
+        plane0 = keep.tile([P, CHUNK], U8, name="plane0", tag="even", align_bytes=64)
+        plane1 = keep.tile([P, CHUNK], U8, name="plane1", align_bytes=64)
         h0 = quantize_hidden(0, plane0[:])
-        out_code = keep.tile([P, 2 * N], U32, name="out_code", align_bytes=64)
-        out_scale = keep.tile([P, 2 * N], U8, name="out_scale", align_bytes=64)
-        nc.vector.quantize_mx(out_code[:].bitcast(FP8X4), out_scale[:], out_bf[:])
-        w3_mx, w1_mx = (out_code[:, 0:N], out_scale[:, 0:N]), (out_code[:, N:], out_scale[:, N:])
-        gather(2)
+        out_code = [
+            reuse.tile([P, 2 * P], U32, name="out_code0", offset=OUT_CODE_AT, align_bytes=64),
+            keep.tile([P, 2 * P], U32, name="out_code1", align_bytes=64),
+        ]
+        out_scale = keep.tile([P, ROW_TILES, 2 * P], U8, name="out_scale", align_bytes=64)
+        for r in range(ROW_TILES):
+            both = out_bf[:, r].rearrange("p w n -> p (w n)")
+            nc.vector.quantize_mx(out_code[r][:].bitcast(FP8X4), out_scale[:, r, :], both)
+        w3_mx, w1_mx = slice(0, P), slice(P, 2 * P)
         h1 = quantize_hidden(CHUNK, plane1[:])
 
+        plane2 = keep.tile([P, CHUNK], U8, name="plane2", tag="even", align_bytes=64)
         acc0 = psum.tile([P, ROW_TILES, CHUNK], F32, name="acc0", tag="bank6")
-        adapter(rows(acc0), h0, opens=(True, False))
-        direct(rows(acc0), 0, CHUNK, closes=(False, True))
-        acc1 = psum.tile([P, ROW_TILES, CHUNK], F32, name="acc1", tag="bank7")
-        direct(rows(acc1), CHUNK, CHUNK, (True, False))
-        hidden_unit(6)
-        adapter(rows(acc1), h1, closes=(False, True))
-        hidden_unit(7)
+        for r in range(ROW_TILES):
+            product(acc0[:, r, :], r, w3_mx, h0, start=r == 0)
+            product(acc0[:, r, :], r, w1_mx, tokens(0, CHUNK), stop=r == ROW_TILES - 1)
+
+        def row_banks(name, banks):
+            return [psum.tile([P, CHUNK], F32, name=f"{name}_{r}", tag=f"bank{banks[r]}")[:] for r in range(ROW_TILES)]
+
+        acc1 = row_banks("acc1", (7, 2))
+        direct(acc1, CHUNK, CHUNK, (True, True))
+        adapter(acc1, h1, closes=(True, True))
         nc.vector.tensor_copy(results[0][:], acc0[:])
         store(0, results[0])
 
-        plane2 = keep.tile([P, CHUNK], U8, name="plane2", align_bytes=64)
         h2 = quantize_hidden(2 * CHUNK, plane2[:])
-        nc.vector.tensor_copy(results[1][:], acc1[:])
+        acc2 = row_banks("acc2", (4, 5))
+        direct(acc2, 2 * CHUNK, CHUNK, (True, True))
+        adapter(acc2, h2, closes=(True, True))
+
+        plane3 = keep.tile([P, CHUNK], U8, name="plane3", align_bytes=64)
+        acc3 = row_banks("acc3", (3, 6))
+        direct(acc3, 3 * CHUNK, CHUNK, (True, True))
+        adapter([acc[:, halves[0]] for acc in acc3], quantize_hidden(3 * CHUNK, plane3[:, halves[0]]))
+        nc.vector.tensor_copy(results[1][:, 0, :], acc1[0])
+        nc.scalar.copy(results[1][:, 1, :], acc1[1])
         store(1, results[1])
-
-        plane3 = keep.tile([P, CHUNK], U8, name="plane3", tag="odd", align_bytes=64)
-        h3 = [quantize_hidden(3 * CHUNK + half.start, plane3[:, half]) for half in halves]
-        acc2 = psum.tile([P, ROW_TILES, CHUNK], F32, name="acc2", tag="bank6")
-        direct(rows(acc2), 2 * CHUNK, CHUNK, (True, False))
-        adapter(rows(acc2), h2, closes=(False, True))
-        nc.scalar.copy(results[2][:], acc2[:])
-        store(2, results[2])
-
-        last = [psum.tile([P, CHUNK], F32, name=f"last{r}", tag=f"bank{2 + r}") for r in range(ROW_TILES)]
-        direct([acc[:] for acc in last], 3 * CHUNK, CHUNK, (True, True))
-        adapter([acc[:, halves[0]] for acc in last], h3[0])
-        adapter([acc[:, halves[1]] for acc in last], h3[1], closes=(True, True))
-        nc.scalar.copy(results[3][:, 0, :], last[0][:])
-        nc.vector.tensor_copy(results[3][:, 1, :], last[1][:])
-        store(3, results[3])
+        h_last = quantize_hidden(3 * CHUNK + UNIT, plane3[:, halves[1]])
+        adapter([acc[:, halves[1]] for acc in acc3], h_last, closes=(True, True))
+        for c, accs in ((2, acc2), (3, acc3)):
+            nc.scalar.copy(results[c][:, 0, :], accs[0])
+            nc.vector.tensor_copy(results[c][:, 1, :], accs[1])
+            store(c, results[c])

@@ -30,14 +30,13 @@ W2_HEAD = 768
 TABLE_ROW0 = 32
 TABLE_STEP = 4
 
-PIECES = (256, 256, 512)
+PIECES = (256, 512, 256)
 
 HIDDEN_AT = 0
 W3_FIRST_AT = 6144
 W3_LAST_AT = 9216
-OUT_CODE_AT = 8256
+LAST_PIECE_AT = 9280
 SECOND_CODE_AT = 10304
-FIRST_PIECE_AT = 12288
 
 
 def side_by_side(grouped, raw):
@@ -110,9 +109,9 @@ def tile_picked_lora_gelu_p_kernel(tc, x_words, x_scales, w1, w2, w3, offs, out)
 
         starts = [sum(PIECES[:n]) for n in range(len(PIECES))]
         x_code = [
-            reuse.tile([P, PIECES[0]], U32, name="x_code0", offset=FIRST_PIECE_AT, align_bytes=64),
+            keep.tile([P, PIECES[0]], U32, name="x_code0", align_bytes=64),
             keep.tile([P, PIECES[1]], U32, name="x_code1", align_bytes=64),
-            keep.tile([P, PIECES[2]], U32, name="x_code2", align_bytes=64),
+            reuse.tile([P, PIECES[2]], U32, name="x_code2", offset=LAST_PIECE_AT, align_bytes=64),
         ]
 
         def gather(n):
@@ -147,23 +146,32 @@ def tile_picked_lora_gelu_p_kernel(tc, x_words, x_scales, w1, w2, w3, offs, out)
 
         gather(0)
         gather(1)
-        gather(2)
-        out_bf = keep.tile([P, ROW_TILES, 2, P * PACK], BF16, name="out_bf", align_bytes=64)
-        nc.scalar.copy(*side_by_side(out_bf[:, 0, 0, :], w3_raw[0][:]))
-        for unit in range(S // UNIT):
+        out_bf = keep.tile([P, 2 * N * PACK], BF16, name="out_bf", align_bytes=64)
+        nc.scalar.copy(*side_by_side(out_bf[:, 0 : P * PACK], w3_raw[0][:]))
+        for unit in range(starts[2] // UNIT):
             hidden_unit(unit)
-        nc.vector.tensor_copy(
-            out_bf[:, :, 1, :].rearrange("p r (c i j) -> p r c j i", i=4, j=PACK),
-            w1_raw[:].rearrange("p (j r c i) -> p r c j i", j=PACK, r=ROW_TILES, i=4),
-        )
-        nc.vector.tensor_copy(*side_by_side(out_bf[:, 1, 0, :], w3_raw[1][:]))
+        w1_rows = w1_raw[:].rearrange("p (j c) -> p j c", j=PACK)
+        nc.vector.tensor_copy(*side_by_side(out_bf[:, P * PACK : 3 * P * PACK], w1_rows))
+        nc.vector.tensor_copy(*side_by_side(out_bf[:, 3 * P * PACK :], w3_raw[1][:]))
+
+        out_code = keep.tile([P, 2 * N], U32, name="out_code", align_bytes=64)
+        out_scale = keep.tile([P, 2 * N], U8, name="out_scale", align_bytes=64)
+        w3_mx, w1_mx = (0, 3), (1, 2)
+
+        def quantize_weights(first, last):
+            cols = slice(first * P, last * P)
+            nc.vector.quantize_mx(
+                out_code[:, cols].bitcast(FP8X4), out_scale[:, cols], out_bf[:, first * P * PACK : last * P * PACK]
+            )
+
+        quantize_weights(0, 3)
 
         out_rows = out.rearrange("(r p) n -> p r n", p=P)
         h_code = [
             keep.tile([P, CHUNK], U32, name="h_code0", align_bytes=64),
             reuse.tile([P, CHUNK], U32, name="h_code1", offset=SECOND_CODE_AT, align_bytes=64),
             keep.tile([P, CHUNK], U32, name="h_code2", align_bytes=64),
-            reuse.tile([P, CHUNK], U32, name="h_code3", offset=FIRST_PIECE_AT, align_bytes=64),
+            keep.tile([P, CHUNK], U32, name="h_code3", align_bytes=64),
         ]
 
         def quantize_hidden(start, plane):
@@ -176,8 +184,8 @@ def tile_picked_lora_gelu_p_kernel(tc, x_words, x_scales, w1, w2, w3, offs, out)
         def product(acc, r, weights, moving, start=False, stop=False):
             nc.tensor.matmul_mx(
                 acc,
-                lhsT=out_code[r][:, weights].bitcast(FP8X4),
-                lhsT_scale=out_scale[:, r, weights],
+                lhsT=out_code[:, weights[r] * P : (weights[r] + 1) * P].bitcast(FP8X4),
+                lhsT_scale=out_scale[:, weights[r] * P : (weights[r] + 1) * P],
                 rhs=moving[0],
                 rhs_scale=moving[1],
                 start=start,
@@ -198,54 +206,51 @@ def tile_picked_lora_gelu_p_kernel(tc, x_words, x_scales, w1, w2, w3, offs, out)
         def rows(acc, cols=slice(None)):
             return [acc[:, r, cols] for r in range(ROW_TILES)]
 
-        results = [keep.tile([P, ROW_TILES, CHUNK], F32, name=f"result{c}") for c in (0, 1)]
-        results.append(reuse.tile([P, ROW_TILES, CHUNK], F32, name="result2", offset=HIDDEN_AT, align_bytes=64))
-        results.append(keep.tile([P, ROW_TILES, CHUNK], F32, name="result3"))
+        results = [keep.tile([P, ROW_TILES, CHUNK], F32, name=f"result{c}") for c in range(S // CHUNK)]
         halves = [slice(0, UNIT), slice(UNIT, CHUNK)]
         plane0 = keep.tile([P, CHUNK], U8, name="plane0", tag="even", align_bytes=64)
-        plane1 = keep.tile([P, CHUNK], U8, name="plane1", align_bytes=64)
+        plane1 = keep.tile([P, CHUNK], U8, name="plane1", tag="odd", align_bytes=64)
         h0 = quantize_hidden(0, plane0[:])
-        out_code = [
-            reuse.tile([P, 2 * P], U32, name="out_code0", offset=OUT_CODE_AT, align_bytes=64),
-            keep.tile([P, 2 * P], U32, name="out_code1", align_bytes=64),
-        ]
-        out_scale = keep.tile([P, ROW_TILES, 2 * P], U8, name="out_scale", align_bytes=64)
-        for r in range(ROW_TILES):
-            both = out_bf[:, r].rearrange("p w n -> p (w n)")
-            nc.vector.quantize_mx(out_code[r][:].bitcast(FP8X4), out_scale[:, r, :], both)
-        w3_mx, w1_mx = slice(0, P), slice(P, 2 * P)
+        quantize_weights(3, 4)
+        gather(2)
         h1 = quantize_hidden(CHUNK, plane1[:])
 
-        plane2 = keep.tile([P, CHUNK], U8, name="plane2", tag="even", align_bytes=64)
         acc0 = psum.tile([P, ROW_TILES, CHUNK], F32, name="acc0", tag="bank6")
-        for r in range(ROW_TILES):
-            product(acc0[:, r, :], r, w3_mx, h0, start=r == 0)
-            product(acc0[:, r, :], r, w1_mx, tokens(0, CHUNK), stop=r == ROW_TILES - 1)
-
-        def row_banks(name, banks):
-            return [psum.tile([P, CHUNK], F32, name=f"{name}_{r}", tag=f"bank{banks[r]}")[:] for r in range(ROW_TILES)]
-
-        acc1 = row_banks("acc1", (7, 2))
-        direct(acc1, CHUNK, CHUNK, (True, True))
-        adapter(acc1, h1, closes=(True, True))
+        direct(rows(acc0), 0, CHUNK, (True, False))
+        adapter(rows(acc0), h0, closes=(False, True))
+        acc1 = psum.tile([P, ROW_TILES, CHUNK], F32, name="acc1", tag="bank7")
+        direct(rows(acc1), CHUNK, CHUNK, (True, False))
+        hidden_unit(6)
+        adapter(rows(acc1), h1, closes=(False, True))
+        hidden_unit(7)
         nc.vector.tensor_copy(results[0][:], acc0[:])
         store(0, results[0])
 
+        plane2 = keep.tile([P, CHUNK], U8, name="plane2", tag="even", align_bytes=64)
         h2 = quantize_hidden(2 * CHUNK, plane2[:])
-        acc2 = row_banks("acc2", (4, 5))
+        nc.vector.tensor_copy(results[1][:], acc1[:])
+        store(1, results[1])
+
+        def row_banks(name, banks, width):
+            return [psum.tile([P, width], F32, name=f"{name}_{r}", tag=f"bank{banks[r]}")[:] for r in range(ROW_TILES)]
+
+        acc2 = row_banks("acc2", (4, 5), CHUNK)
         direct(acc2, 2 * CHUNK, CHUNK, (True, True))
         adapter(acc2, h2, closes=(True, True))
-
-        plane3 = keep.tile([P, CHUNK], U8, name="plane3", align_bytes=64)
-        acc3 = row_banks("acc3", (3, 6))
-        direct(acc3, 3 * CHUNK, CHUNK, (True, True))
-        adapter([acc[:, halves[0]] for acc in acc3], quantize_hidden(3 * CHUNK, plane3[:, halves[0]]))
-        nc.vector.tensor_copy(results[1][:, 0, :], acc1[0])
-        nc.scalar.copy(results[1][:, 1, :], acc1[1])
-        store(1, results[1])
+        plane3 = keep.tile([P, CHUNK], U8, name="plane3", tag="odd", align_bytes=64)
+        h_sixth = quantize_hidden(3 * CHUNK, plane3[:, halves[0]])
+        nc.vector.tensor_copy(results[2][:, 0, :], acc2[0])
+        nc.scalar.copy(results[2][:, 1, :], acc2[1])
+        store(2, results[2])
         h_last = quantize_hidden(3 * CHUNK + UNIT, plane3[:, halves[1]])
-        adapter([acc[:, halves[1]] for acc in acc3], h_last, closes=(True, True))
-        for c, accs in ((2, acc2), (3, acc3)):
-            nc.scalar.copy(results[c][:, 0, :], accs[0])
-            nc.vector.tensor_copy(results[c][:, 1, :], accs[1])
-            store(c, results[c])
+
+        acc3 = psum.tile([P, ROW_TILES, UNIT], F32, name="acc3", tag="bank6")
+        direct(rows(acc3), 3 * CHUNK, UNIT, (True, False))
+        adapter(rows(acc3), h_sixth, closes=(False, True))
+        last = row_banks("last", (2, 3), UNIT)
+        direct(last, 3 * CHUNK + UNIT, UNIT, (True, True))
+        adapter(last, h_last, closes=(True, True))
+        nc.scalar.copy(results[3][:, :, halves[0]], acc3[:])
+        nc.scalar.copy(results[3][:, 0, halves[1]], last[0])
+        nc.vector.tensor_copy(results[3][:, 1, halves[1]], last[1])
+        store(3, results[3])

@@ -22,21 +22,16 @@ SCALE_ROWS = 16
 HALF = S // 2
 UNIT = 128
 ROW_TILES = N // P
-W2_SCALAR = 72
 WARM_UPS = 4
 WARM_UP_ROWS = 32
 CHUNK = 256
-W2_HEAD = 768
 TABLE_ROW0 = 32
 TABLE_STEP = 4
 
 PIECES = (256, 512, 256)
 
-HIDDEN_AT = 0
-W3_FIRST_AT = 6144
-W3_LAST_AT = 9216
-LAST_PIECE_AT = 9280
-SECOND_CODE_AT = 10304
+W1_RAW_AT = 0
+W1_ROUNDED_AT = 4096
 
 
 def side_by_side(grouped, raw):
@@ -55,13 +50,16 @@ def tile_picked_lora_gelu_p_kernel(tc, x_words, x_scales, w1, w2, w3, offs, out)
         nc.vector.memset(table_words, 0)
         w2_raw = keep.tile([P, PACK * H], F32, name="w2_raw")
         w2_rows = w2.rearrange("(p j) c -> p (j c)", j=PACK)
-        nc.sync.dma_start(w2_raw[:, 0:W2_HEAD], w2_rows[:, 0:W2_HEAD])
         offsets = keep.tile([P, S // LIST_ROWS], U16, name="offsets")
         nc.sync.dma_start(offsets[:], offs)
+        nc.sync.dma_start(w2_raw[:], w2_rows)
         nc.sync.dma_start(table_words[TABLE_ROW0 : TABLE_ROW0 + TABLE_STEP * SCALE_ROWS : TABLE_STEP, :], x_scales[0].bitcast(I32))
-        nc.sync.dma_start(w2_raw[:, W2_HEAD:], w2_rows[:, W2_HEAD:])
         word_table = keep.tile([P, T], I32, name="word_table", align_bytes=64)
         nc.sync.dma_start(word_table[:], x_words[0].rearrange("p n t -> p (n t)").bitcast(I32))
+
+        w3_rows = w3.rearrange("(p j) c -> p j c", j=PACK)
+        w3_raw = [keep.tile([P, PACK, P], F32, name=f"w3_raw{r}", align_bytes=64) for r in range(ROW_TILES)]
+        nc.sync.dma_start(w3_raw[0][:], w3_rows[:, :, 0:P])
 
         warm = keep.tile([P, 2], F32, name="warm")
         nc.vector.memset(warm[:, 0:1], 0.0)
@@ -76,21 +74,14 @@ def tile_picked_lora_gelu_p_kernel(tc, x_words, x_scales, w1, w2, w3, offs, out)
             rows_r = slice(first, first + TABLE_STEP * PACK * 3 + 1, TABLE_STEP * PACK)
             nc.sync.dma_start(x_scale[r:P:QUADRANT, :].bitcast(I32), spread_scale[rows_r, :].bitcast(I32))
 
-        w3_rows = w3.rearrange("(p j) c -> p j c", j=PACK)
-        w3_raw = [
-            reuse.tile([P, PACK, P], F32, name="w3_raw0", offset=W3_FIRST_AT, align_bytes=64),
-            reuse.tile([P, PACK, P], F32, name="w3_raw1", offset=W3_LAST_AT, align_bytes=64),
-        ]
-        w1_raw = keep.tile([P, PACK * N], F32, name="w1_raw", align_bytes=64)
-        nc.sync.dma_start(w3_raw[0][:], w3_rows[:, :, 0:P])
+        w1_raw = reuse.tile([P, PACK * N], F32, name="w1_raw", offset=W1_RAW_AT, align_bytes=64)
         nc.sync.dma_start(w1_raw[:], w1.rearrange("(p j) c -> p (j c)", j=PACK))
         nc.sync.dma_start(w3_raw[1][:], w3_rows[:, :, P:N])
 
         w2_bf = keep.tile([P, PACK * H], BF16, name="w2_bf", align_bytes=64)
         dealt = w2_bf[:].rearrange("p (t m j) -> p m t j", t=PACK, j=PACK)
         undealt = w2_raw[:].rearrange("p (j m t) -> p m t j", j=PACK, t=PACK)
-        nc.scalar.copy(dealt[:, 0:W2_SCALAR], undealt[:, 0:W2_SCALAR])
-        nc.vector.tensor_copy(dealt[:, W2_SCALAR:P], undealt[:, W2_SCALAR:P])
+        nc.scalar.copy(dealt, undealt)
         w2_code = keep.tile([P, H], U32, name="w2_code", align_bytes=64)
         w2_scale = keep.tile([P, H], U8, name="w2_scale", align_bytes=64)
         nc.vector.quantize_mx(w2_code[:].bitcast(FP8X4), w2_scale[:], w2_bf[:])
@@ -111,7 +102,7 @@ def tile_picked_lora_gelu_p_kernel(tc, x_words, x_scales, w1, w2, w3, offs, out)
         x_code = [
             keep.tile([P, PIECES[0]], U32, name="x_code0", align_bytes=64),
             keep.tile([P, PIECES[1]], U32, name="x_code1", align_bytes=64),
-            reuse.tile([P, PIECES[2]], U32, name="x_code2", offset=LAST_PIECE_AT, align_bytes=64),
+            reuse.tile([P, PIECES[2]], U32, name="x_code2", offset=W1_ROUNDED_AT, align_bytes=64),
         ]
 
         def gather(n):
@@ -123,7 +114,7 @@ def tile_picked_lora_gelu_p_kernel(tc, x_words, x_scales, w1, w2, w3, offs, out)
             at = start - starts[n]
             return x_code[n][:, at : at + width].bitcast(FP8X4), x_scale[:, start : start + width]
 
-        h_bf = reuse.tile([P, S * PACK], BF16, name="h_bf", offset=HIDDEN_AT, align_bytes=64)
+        h_bf = keep.tile([P, S * PACK], BF16, name="h_bf", align_bytes=64)
 
         def hidden_unit(unit):
             bank = psum.tile([P, PACK, UNIT], F32, name="h_bank", tag=f"bank{unit % 6}")
@@ -146,30 +137,34 @@ def tile_picked_lora_gelu_p_kernel(tc, x_words, x_scales, w1, w2, w3, offs, out)
 
         gather(0)
         gather(1)
-        out_bf = keep.tile([P, 2 * N * PACK], BF16, name="out_bf", align_bytes=64)
-        nc.scalar.copy(*side_by_side(out_bf[:, 0 : P * PACK], w3_raw[0][:]))
+        w3_bf = [keep.tile([P, P * PACK], BF16, name=f"w3_bf{r}", align_bytes=64) for r in range(ROW_TILES)]
+        w1_bf = [
+            keep.tile([P, P * PACK], BF16, name="w1_bf0", align_bytes=64),
+            reuse.tile([P, P * PACK], BF16, name="w1_bf1", offset=W1_ROUNDED_AT + 2 * CHUNK, align_bytes=64),
+        ]
+        out_code = keep.tile([P, 2 * N], U32, name="out_code", align_bytes=64)
+        out_scale = keep.tile([P, 2 * N], U8, name="out_scale", align_bytes=64)
+        w3_mx, w1_mx = (0, 1), (2, 3)
+
+        def quantize_weights(place, rounded):
+            cols = slice(place * P, (place + 1) * P)
+            nc.vector.quantize_mx(out_code[:, cols].bitcast(FP8X4), out_scale[:, cols], rounded[:])
+
+        nc.scalar.copy(*side_by_side(w3_bf[0][:], w3_raw[0][:]))
+        quantize_weights(w3_mx[0], w3_bf[0])
         for unit in range(starts[2] // UNIT):
             hidden_unit(unit)
         w1_rows = w1_raw[:].rearrange("p (j c) -> p j c", j=PACK)
-        nc.vector.tensor_copy(*side_by_side(out_bf[:, P * PACK : 3 * P * PACK], w1_rows))
-        nc.vector.tensor_copy(*side_by_side(out_bf[:, 3 * P * PACK :], w3_raw[1][:]))
-
-        out_code = keep.tile([P, 2 * N], U32, name="out_code", align_bytes=64)
-        out_scale = keep.tile([P, 2 * N], U8, name="out_scale", align_bytes=64)
-        w3_mx, w1_mx = (0, 3), (1, 2)
-
-        def quantize_weights(first, last):
-            cols = slice(first * P, last * P)
-            nc.vector.quantize_mx(
-                out_code[:, cols].bitcast(FP8X4), out_scale[:, cols], out_bf[:, first * P * PACK : last * P * PACK]
-            )
-
-        quantize_weights(0, 3)
+        for r in range(ROW_TILES):
+            nc.vector.tensor_copy(*side_by_side(w1_bf[r][:], w1_rows[:, :, r * P : (r + 1) * P]))
+        quantize_weights(w1_mx[0], w1_bf[0])
+        nc.vector.tensor_copy(*side_by_side(w3_bf[1][:], w3_raw[1][:]))
+        quantize_weights(w1_mx[1], w1_bf[1])
 
         out_rows = out.rearrange("(r p) n -> p r n", p=P)
         h_code = [
-            keep.tile([P, CHUNK], U32, name="h_code0", align_bytes=64),
-            reuse.tile([P, CHUNK], U32, name="h_code1", offset=SECOND_CODE_AT, align_bytes=64),
+            reuse.tile([P, CHUNK], U32, name="h_code0", offset=W1_RAW_AT, align_bytes=64),
+            reuse.tile([P, CHUNK], U32, name="h_code1", offset=W1_ROUNDED_AT + 4 * CHUNK, align_bytes=64),
             keep.tile([P, CHUNK], U32, name="h_code2", align_bytes=64),
             keep.tile([P, CHUNK], U32, name="h_code3", align_bytes=64),
         ]
@@ -192,8 +187,8 @@ def tile_picked_lora_gelu_p_kernel(tc, x_words, x_scales, w1, w2, w3, offs, out)
                 stop=stop,
             )
 
-        def store(c, result):
-            nc.sync.dma_start(out_rows[:, :, c * CHUNK : (c + 1) * CHUNK], result[:])
+        def store(c, result, cols=slice(0, CHUNK)):
+            nc.sync.dma_start(out_rows[:, :, c * CHUNK + cols.start : c * CHUNK + cols.stop], result[:, :, cols])
 
         def direct(accs, start, width, opens=(False, False), closes=(False, False)):
             for r in range(ROW_TILES):
@@ -211,7 +206,7 @@ def tile_picked_lora_gelu_p_kernel(tc, x_words, x_scales, w1, w2, w3, offs, out)
         plane0 = keep.tile([P, CHUNK], U8, name="plane0", tag="even", align_bytes=64)
         plane1 = keep.tile([P, CHUNK], U8, name="plane1", tag="odd", align_bytes=64)
         h0 = quantize_hidden(0, plane0[:])
-        quantize_weights(3, 4)
+        quantize_weights(w3_mx[1], w3_bf[1])
         gather(2)
         h1 = quantize_hidden(CHUNK, plane1[:])
 
@@ -234,13 +229,12 @@ def tile_picked_lora_gelu_p_kernel(tc, x_words, x_scales, w1, w2, w3, offs, out)
         def row_banks(name, banks, width):
             return [psum.tile([P, width], F32, name=f"{name}_{r}", tag=f"bank{banks[r]}")[:] for r in range(ROW_TILES)]
 
-        acc2 = row_banks("acc2", (4, 5), CHUNK)
-        direct(acc2, 2 * CHUNK, CHUNK, (True, True))
-        adapter(acc2, h2, closes=(True, True))
+        acc2 = psum.tile([P, ROW_TILES, CHUNK], F32, name="acc2", tag="bank4")
+        direct(rows(acc2), 2 * CHUNK, CHUNK, (True, False))
+        adapter(rows(acc2), h2, closes=(False, True))
         plane3 = keep.tile([P, CHUNK], U8, name="plane3", tag="odd", align_bytes=64)
         h_sixth = quantize_hidden(3 * CHUNK, plane3[:, halves[0]])
-        nc.vector.tensor_copy(results[2][:, 0, :], acc2[0])
-        nc.scalar.copy(results[2][:, 1, :], acc2[1])
+        nc.scalar.copy(results[2][:], acc2[:])
         store(2, results[2])
         h_last = quantize_hidden(3 * CHUNK + UNIT, plane3[:, halves[1]])
 
@@ -250,7 +244,8 @@ def tile_picked_lora_gelu_p_kernel(tc, x_words, x_scales, w1, w2, w3, offs, out)
         last = row_banks("last", (2, 3), UNIT)
         direct(last, 3 * CHUNK + UNIT, UNIT, (True, True))
         adapter(last, h_last, closes=(True, True))
-        nc.scalar.copy(results[3][:, :, halves[0]], acc3[:])
+        nc.vector.tensor_copy(results[3][:, :, halves[0]], acc3[:])
+        store(3, results[3], halves[0])
         nc.scalar.copy(results[3][:, 0, halves[1]], last[0])
         nc.vector.tensor_copy(results[3][:, 1, halves[1]], last[1])
-        store(3, results[3])
+        store(3, results[3], halves[1])

@@ -25,6 +25,8 @@ ROW_TILES = N // P
 WARM_UPS = 4
 WARM_UP_ROWS = 32
 CHUNK = 256
+W2_HEAD = 768
+W2_SCALAR = 72
 TABLE_ROW0 = 32
 TABLE_STEP = 4
 
@@ -50,10 +52,11 @@ def tile_picked_lora_gelu_p_kernel(tc, x_words, x_scales, w1, w2, w3, offs, out)
         nc.vector.memset(table_words, 0)
         w2_raw = keep.tile([P, PACK * H], F32, name="w2_raw")
         w2_rows = w2.rearrange("(p j) c -> p (j c)", j=PACK)
+        nc.sync.dma_start(w2_raw[:, 0:W2_HEAD], w2_rows[:, 0:W2_HEAD])
         offsets = keep.tile([P, S // LIST_ROWS], U16, name="offsets")
         nc.sync.dma_start(offsets[:], offs)
-        nc.sync.dma_start(w2_raw[:], w2_rows)
         nc.sync.dma_start(table_words[TABLE_ROW0 : TABLE_ROW0 + TABLE_STEP * SCALE_ROWS : TABLE_STEP, :], x_scales[0].bitcast(I32))
+        nc.sync.dma_start(w2_raw[:, W2_HEAD:], w2_rows[:, W2_HEAD:])
         word_table = keep.tile([P, T], I32, name="word_table", align_bytes=64)
         nc.sync.dma_start(word_table[:], x_words[0].rearrange("p n t -> p (n t)").bitcast(I32))
 
@@ -81,7 +84,8 @@ def tile_picked_lora_gelu_p_kernel(tc, x_words, x_scales, w1, w2, w3, offs, out)
         w2_bf = keep.tile([P, PACK * H], BF16, name="w2_bf", align_bytes=64)
         dealt = w2_bf[:].rearrange("p (t m j) -> p m t j", t=PACK, j=PACK)
         undealt = w2_raw[:].rearrange("p (j m t) -> p m t j", j=PACK, t=PACK)
-        nc.scalar.copy(dealt, undealt)
+        nc.scalar.copy(dealt[:, 0:W2_SCALAR], undealt[:, 0:W2_SCALAR])
+        nc.vector.tensor_copy(dealt[:, W2_SCALAR:P], undealt[:, W2_SCALAR:P])
         w2_code = keep.tile([P, H], U32, name="w2_code", align_bytes=64)
         w2_scale = keep.tile([P, H], U8, name="w2_scale", align_bytes=64)
         nc.vector.quantize_mx(w2_code[:].bitcast(FP8X4), w2_scale[:], w2_bf[:])
@@ -187,8 +191,8 @@ def tile_picked_lora_gelu_p_kernel(tc, x_words, x_scales, w1, w2, w3, offs, out)
                 stop=stop,
             )
 
-        def store(c, result, cols=slice(0, CHUNK)):
-            nc.sync.dma_start(out_rows[:, :, c * CHUNK + cols.start : c * CHUNK + cols.stop], result[:, :, cols])
+        def store(c, result):
+            nc.sync.dma_start(out_rows[:, :, c * CHUNK : (c + 1) * CHUNK], result[:])
 
         def direct(accs, start, width, opens=(False, False), closes=(False, False)):
             for r in range(ROW_TILES):
@@ -245,7 +249,6 @@ def tile_picked_lora_gelu_p_kernel(tc, x_words, x_scales, w1, w2, w3, offs, out)
         direct(last, 3 * CHUNK + UNIT, UNIT, (True, True))
         adapter(last, h_last, closes=(True, True))
         nc.vector.tensor_copy(results[3][:, :, halves[0]], acc3[:])
-        store(3, results[3], halves[0])
         nc.scalar.copy(results[3][:, 0, halves[1]], last[0])
         nc.vector.tensor_copy(results[3][:, 1, halves[1]], last[1])
-        store(3, results[3], halves[1])
+        store(3, results[3])

@@ -82,8 +82,8 @@ def tile_picked_lora_gelu_p_kernel(tc, x_words, x_scales, w1, w2, w3, offs, out)
         nc.sync.dma_start(w3_raw[1][:], w3_rows[:, :, P:N])
 
         w2_bf = keep.tile([P, PACK * H], BF16, name="w2_bf", align_bytes=64)
-        dealt = w2_bf[:].rearrange("p (t m j) -> p m t j", t=PACK, j=PACK)
-        undealt = w2_raw[:].rearrange("p (j m t) -> p m t j", j=PACK, t=PACK)
+        dealt = w2_bf[:].rearrange("p (t m j) -> p m j t", t=PACK, j=PACK)
+        undealt = w2_raw[:].rearrange("p (j m t) -> p m j t", j=PACK, t=PACK)
         nc.scalar.copy(dealt[:, 0:W2_SCALAR], undealt[:, 0:W2_SCALAR])
         nc.vector.tensor_copy(dealt[:, W2_SCALAR:P], undealt[:, W2_SCALAR:P])
         w2_code = keep.tile([P, H], U32, name="w2_code", align_bytes=64)

from contextlib import ExitStack

import concourse.mybir as mybir

K, T, S, H, N = 512, 4096, 1024, 512, 256
FLOPS = 2 * S * (K * H + K * N + H * N)

F32 = mybir.dt.float32
BF16 = mybir.dt.bfloat16
I32 = mybir.dt.int32
U32 = mybir.dt.uint32
U16 = mybir.dt.uint16
U8 = mybir.dt.uint8
FP8X4 = mybir.dt.float8_e4m3fn_x4
GELU = mybir.ActivationFunctionType.Gelu_apprx_tanh

P = 128
PACK = 4
LIST_ROWS = 16
QUADRANT = 32
SCALE_ROWS = 16
HALF = S // 2
UNIT = 128
ROW_TILES = N // P
WARM_UPS = 4
WARM_UP_ROWS = 32
CHUNK = 256
W2_HEAD = 768
W2_SCALAR = 72
TABLE_ROW0 = 32
TABLE_STEP = 4

PIECES = (256, 512, 256)

W1_RAW_AT = 0
W1_ROUNDED_AT = 4096


def side_by_side(grouped, raw):
    return grouped.rearrange("p (c i j) -> p c j i", i=4, j=PACK), raw.rearrange("p j (c i) -> p c j i", i=4)


def tile_picked_lora_gelu_p_kernel(tc, x_words, x_scales, w1, w2, w3, offs, out):
    nc = tc.nc
    with ExitStack() as ctx:
        keep = ctx.enter_context(tc.tile_pool(name="keep", bufs=1))
        reuse = ctx.enter_context(tc.tile_pool(name="reuse", bufs=1))
        psum = ctx.enter_context(tc.psum_pool(name="psum", bufs=1))

        scale_table = keep.tile([P, T], U8, name="scale_table", align_bytes=64)
        table_words = scale_table[:].bitcast(I32)
        nc.vector.memset(table_words, 0)
        w2_raw = keep.tile([P, PACK * H], F32, name="w2_raw")
        w2_rows = w2.rearrange("(p j) c -> p (j c)", j=PACK)
        nc.sync.dma_start(w2_raw[:, 0:W2_HEAD], w2_rows[:, 0:W2_HEAD])
        offsets = keep.tile([P, S // LIST_ROWS], U16, name="offsets")
        nc.sync.dma_start(offsets[:], offs)
        nc.sync.dma_start(table_words[TABLE_ROW0 : TABLE_ROW0 + TABLE_STEP * SCALE_ROWS : TABLE_STEP, :], x_scales[0].bitcast(I32))
        nc.sync.dma_start(w2_raw[:, W2_HEAD:], w2_rows[:, W2_HEAD:])
        word_table = keep.tile([P, T], I32, name="word_table", align_bytes=64)
        nc.sync.dma_start(word_table[:], x_words[0].rearrange("p n t -> p (n t)").bitcast(I32))

        w3_rows = w3.rearrange("(p j) c -> p j c", j=PACK)
        w3_raw = [keep.tile([P, PACK, P], F32, name=f"w3_raw{r}", align_bytes=64) for r in range(ROW_TILES)]
        nc.sync.dma_start(w3_raw[0][:], w3_rows[:, :, 0:P])

        warm = keep.tile([P, 2], F32, name="warm")
        nc.vector.memset(warm[:, 0:1], 0.0)
        nc.scalar.activation(warm[:, 1:2], warm[:, 0:1], GELU)

        x_scale = keep.tile([P, S], U8, name="x_scale", align_bytes=64)
        nc.vector.memset(x_scale[:].bitcast(I32), 0)
        spread_scale = keep.tile([P, S], U8, name="spread_scale", align_bytes=64)
        nc.vector.tensor_copy(spread_scale[:], scale_table[:].indirect(offsets[:]))
        for r in range(PACK):
            first = TABLE_ROW0 + TABLE_STEP * r
            rows_r = slice(first, first + TABLE_STEP * PACK * 3 + 1, TABLE_STEP * PACK)
            nc.sync.dma_start(x_scale[r:P:QUADRANT, :].bitcast(I32), spread_scale[rows_r, :].bitcast(I32))

        w1_raw = reuse.tile([P, PACK * N], F32, name="w1_raw", offset=W1_RAW_AT, align_bytes=64)
        nc.sync.dma_start(w1_raw[:], w1.rearrange("(p j) c -> p (j c)", j=PACK))
        nc.sync.dma_start(w3_raw[1][:], w3_rows[:, :, P:N])

        w2_bf = keep.tile([P, PACK * H], BF16, name="w2_bf", align_bytes=64)
        dealt = w2_bf[:].rearrange("p (t m j) -> p m j t", t=PACK, j=PACK)
        undealt = w2_raw[:].rearrange("p (j m t) -> p m j t", j=PACK, t=PACK)
        nc.scalar.copy(dealt[:, 0:W2_SCALAR], undealt[:, 0:W2_SCALAR])
        nc.vector.tensor_copy(dealt[:, W2_SCALAR:P], undealt[:, W2_SCALAR:P])
        w2_code = keep.tile([P, H], U32, name="w2_code", align_bytes=64)
        w2_scale = keep.tile([P, H], U8, name="w2_scale", align_bytes=64)
        nc.vector.quantize_mx(w2_code[:].bitcast(FP8X4), w2_scale[:], w2_bf[:])

        idle = psum.tile([P, H], F32, name="idle", tag="bank7")
        for turn in range(WARM_UPS):
            nc.tensor.matmul_mx(
                idle[0:WARM_UP_ROWS, :],
                lhsT=w2_code[:, 0:WARM_UP_ROWS].bitcast(FP8X4),
                lhsT_scale=w2_scale[:, 0:WARM_UP_ROWS],
                rhs=w2_code[:].bitcast(FP8X4),
                rhs_scale=w2_scale[:],
                start=True,
                stop=True,
            )

        starts = [sum(PIECES[:n]) for n in range(len(PIECES))]
        x_code = [
            keep.tile([P, PIECES[0]], U32, name="x_code0", align_bytes=64),
            keep.tile([P, PIECES[1]], U32, name="x_code1", align_bytes=64),
            reuse.tile([P, PIECES[2]], U32, name="x_code2", offset=W1_ROUNDED_AT, align_bytes=64),
        ]

        def gather(n):
            entries = offsets[:, starts[n] // LIST_ROWS : (starts[n] + PIECES[n]) // LIST_ROWS]
            nc.vector.tensor_copy(x_code[n][:], word_table[:].bitcast(U32).indirect(entries))

        def tokens(start, width):
            n = max(i for i in range(len(PIECES)) if starts[i] <= start)
            at = start - starts[n]
            return x_code[n][:, at : at + width].bitcast(FP8X4), x_scale[:, start : start + width]

        h_bf = keep.tile([P, S * PACK], BF16, name="h_bf", align_bytes=64)

        def hidden_unit(unit):
            bank = psum.tile([P, PACK, UNIT], F32, name="h_bank", tag=f"bank{unit % 6}")
            code, scale = tokens(unit * UNIT, UNIT)
            for t in range(PACK):
                nc.tensor.matmul_mx(
                    bank[:, t, :],
                    lhsT=w2_code[:, t * P : (t + 1) * P].bitcast(FP8X4),
                    lhsT_scale=w2_scale[:, t * P : (t + 1) * P],
                    rhs=code,
                    rhs_scale=scale,
                    start=True,
                    stop=True,
                )
            nc.scalar.activation(
                h_bf[:, unit * UNIT * PACK : (unit + 1) * UNIT * PACK].rearrange("p (c i t) -> p c t i", i=2, t=PACK),
                bank[:].rearrange("p t (c i) -> p c t i", i=2),
                GELU,
            )

        gather(0)
        gather(1)
        w3_bf = [keep.tile([P, P * PACK], BF16, name=f"w3_bf{r}", align_bytes=64) for r in range(ROW_TILES)]
        w1_bf = [
            keep.tile([P, P * PACK], BF16, name="w1_bf0", align_bytes=64),
            reuse.tile([P, P * PACK], BF16, name="w1_bf1", offset=W1_ROUNDED_AT + 2 * CHUNK, align_bytes=64),
        ]
        out_code = keep.tile([P, 2 * N], U32, name="out_code", align_bytes=64)
        out_scale = keep.tile([P, 2 * N], U8, name="out_scale", align_bytes=64)
        w3_mx, w1_mx = (0, 1), (2, 3)

        def quantize_weights(place, rounded):
            cols = slice(place * P, (place + 1) * P)
            nc.vector.quantize_mx(out_code[:, cols].bitcast(FP8X4), out_scale[:, cols], rounded[:])

        nc.scalar.copy(*side_by_side(w3_bf[0][:], w3_raw[0][:]))
        quantize_weights(w3_mx[0], w3_bf[0])
        for unit in range(starts[2] // UNIT):
            hidden_unit(unit)
        w1_rows = w1_raw[:].rearrange("p (j c) -> p j c", j=PACK)
        for r in range(ROW_TILES):
            nc.vector.tensor_copy(*side_by_side(w1_bf[r][:], w1_rows[:, :, r * P : (r + 1) * P]))
        quantize_weights(w1_mx[0], w1_bf[0])
        nc.vector.tensor_copy(*side_by_side(w3_bf[1][:], w3_raw[1][:]))
        quantize_weights(w1_mx[1], w1_bf[1])

        out_rows = out.rearrange("(r p) n -> p r n", p=P)
        h_code = [
            reuse.tile([P, CHUNK], U32, name="h_code0", offset=W1_RAW_AT, align_bytes=64),
            reuse.tile([P, CHUNK], U32, name="h_code1", offset=W1_ROUNDED_AT + 4 * CHUNK, align_bytes=64),
            keep.tile([P, CHUNK], U32, name="h_code2", align_bytes=64),
            keep.tile([P, CHUNK], U32, name="h_code3", align_bytes=64),
        ]

        def quantize_hidden(start, plane):
            width = plane.shape[1]
            c, at = divmod(start, CHUNK)
            code = h_code[c][:, at : at + width].bitcast(FP8X4)
            nc.vector.quantize_mx(code, plane, h_bf[:, start * PACK : (start + width) * PACK])
            return code, plane

        def product(acc, r, weights, moving, start=False, stop=False):
            nc.tensor.matmul_mx(
                acc,
                lhsT=out_code[:, weights[r] * P : (weights[r] + 1) * P].bitcast(FP8X4),
                lhsT_scale=out_scale[:, weights[r] * P : (weights[r] + 1) * P],
                rhs=moving[0],
                rhs_scale=moving[1],
                start=start,
                stop=stop,
            )

        def store(c, result):
            nc.sync.dma_start(out_rows[:, :, c * CHUNK : (c + 1) * CHUNK], result[:])

        def direct(accs, start, width, opens=(False, False), closes=(False, False)):
            for r in range(ROW_TILES):
                product(accs[r], r, w1_mx, tokens(start, width), start=opens[r], stop=closes[r])

        def adapter(accs, hidden, opens=(False, False), closes=(False, False)):
            for r in range(ROW_TILES):
                product(accs[r], r, w3_mx, hidden, start=opens[r], stop=closes[r])

        def rows(acc, cols=slice(None)):
            return [acc[:, r, cols] for r in range(ROW_TILES)]

        results = [keep.tile([P, ROW_TILES, CHUNK], F32, name=f"result{c}") for c in range(S // CHUNK)]
        halves = [slice(0, UNIT), slice(UNIT, CHUNK)]
        plane0 = keep.tile([P, CHUNK], U8, name="plane0", tag="even", align_bytes=64)
        plane1 = keep.tile([P, CHUNK], U8, name="plane1", tag="odd", align_bytes=64)
        h0 = quantize_hidden(0, plane0[:])
        quantize_weights(w3_mx[1], w3_bf[1])
        gather(2)
        h1 = quantize_hidden(CHUNK, plane1[:])

        acc0 = psum.tile([P, ROW_TILES, CHUNK], F32, name="acc0", tag="bank6")
        direct(rows(acc0), 0, CHUNK, (True, False))
        adapter(rows(acc0), h0, closes=(False, True))
        acc1 = psum.tile([P, ROW_TILES, CHUNK], F32, name="acc1", tag="bank7")
        direct(rows(acc1), CHUNK, CHUNK, (True, False))
        hidden_unit(6)
        adapter(rows(acc1), h1, closes=(False, True))
        hidden_unit(7)
        nc.vector.tensor_copy(results[0][:], acc0[:])
        store(0, results[0])

        plane2 = keep.tile([P, CHUNK], U8, name="plane2", tag="even", align_bytes=64)
        h2 = quantize_hidden(2 * CHUNK, plane2[:])
        nc.vector.tensor_copy(results[1][:], acc1[:])
        store(1, results[1])

        def row_banks(name, banks, width):
            return [psum.tile([P, width], F32, name=f"{name}_{r}", tag=f"bank{banks[r]}")[:] for r in range(ROW_TILES)]

        acc2 = psum.tile([P, ROW_TILES, CHUNK], F32, name="acc2", tag="bank4")
        direct(rows(acc2), 2 * CHUNK, CHUNK, (True, False))
        adapter(rows(acc2), h2, closes=(False, True))
        plane3 = keep.tile([P, CHUNK], U8, name="plane3", tag="odd", align_bytes=64)
        h_sixth = quantize_hidden(3 * CHUNK, plane3[:, halves[0]])
        nc.scalar.copy(results[2][:], acc2[:])
        store(2, results[2])
        h_last = quantize_hidden(3 * CHUNK + UNIT, plane3[:, halves[1]])

        acc3 = psum.tile([P, ROW_TILES, UNIT], F32, name="acc3", tag="bank6")
        direct(rows(acc3), 3 * CHUNK, UNIT, (True, False))
        adapter(rows(acc3), h_sixth, closes=(False, True))
        last = row_banks("last", (2, 3), UNIT)
        direct(last, 3 * CHUNK + UNIT, UNIT, (True, True))
        adapter(last, h_last, closes=(True, True))
        nc.vector.tensor_copy(results[3][:, :, halves[0]], acc3[:])
        nc.scalar.copy(results[3][:, 0, halves[1]], last[0])
        nc.vector.tensor_copy(results[3][:, 1, halves[1]], last[1])
        store(3, results[3])
